import numpy as np, ml_dtypes
CORES = [1,5,17,21,33,37,49,53]
N = 8
import mx_ref
BF = ml_dtypes.bfloat16
def gentries(a):
    return np.ascontiguousarray(a.reshape(8, 16, -1).transpose(0, 2, 1)).reshape(8, -1)
def gtable(e):
    e = np.asarray(e); return np.ascontiguousarray(e.reshape(8, -1, 16).transpose(0, 2, 1)).reshape(128, -1).astype(np.int32)
def gcols(t, e):
    v = np.concatenate([t.reshape(8, 16, -1, 4), np.zeros((8, 16, 1, 4), BF)], axis=2)
    return np.ascontiguousarray(np.stack([v[g][:, e[g]] for g in range(8)])).reshape(128, -1)
def tile(rs):
    return np.stack(rs, axis=2).reshape(128, -1).astype(BF)
def pick(q, e):
    c = np.concatenate([q[0].reshape(128, -1, 4), np.zeros((128, 1, 4), np.uint8)], axis=1); s = np.concatenate([q[1], np.ones((16, 1), np.uint8)], axis=1)
    return (np.ascontiguousarray(c[:, e].reshape(128, -1)), np.ascontiguousarray(s[:, e]))
def join(*qs):
    return (np.concatenate([q[0] for q in qs], axis=1), np.concatenate([q[1] for q in qs], axis=1))
def put(q, e, v):
    c, s = q[0].reshape(128, -1, 4).copy(), q[1].copy(); c[:, e] = v[0].reshape(128, -1, 4); s[:, e] = v[1]
    return (c.reshape(128, -1), s)
def pk(c, s):
    return (np.ascontiguousarray(c), mx_ref.live(s))
def emit(q):
    return q[0], q[1]
def packed(v, rng):
    q = [mx_ref.quantize(np.ascontiguousarray(v[r])) for r in range(N)]
    return np.stack([a for a, b in q]), np.stack([mx_ref.plane(b, rng) for a, b in q])
def values_of_codes():
    e, c = np.zeros((128, 128, 4), np.float32), np.zeros((128, 2, 4), np.uint8)
    e[np.arange(128), np.arange(128), 0] = 1
    c[:127, :, 0] = np.arange(256).reshape(2, 128).T[:127]
    return mx_ref.matmul(mx_ref.quantize(e.reshape(128, 512).astype(BF)), (c.reshape(128, 8), np.full((16, 2), 127, np.uint8))).T.reshape(-1).astype(np.float64)
CODE_VALUE, SCALE_VALUE = values_of_codes(), 2.0 ** (np.arange(256) - 127.0)
def decode(q):
    return (CODE_VALUE[q[0]].reshape(16, 8, -1, 4) * SCALE_VALUE[q[1]][:, None, :, None] + 0.0).reshape(128, -1).astype(np.float32)
def f(rng, *shape):
    return mx_ref.flush((rng.standard_normal(shape, dtype=np.float32) * np.exp2(rng.integers(-2, 3, shape[:-1] + (1,)))).astype(BF))
def wide(rng, *shape, cols=0):
    v = rng.standard_normal(shape, dtype=np.float32) * np.exp2(rng.integers(-12, 13, shape)).astype(np.float32)
    if cols: v *= np.repeat(np.exp2(rng.integers(-cols, cols + 1, shape[:-2] + (1, shape[-1] // 4))) * (rng.random(shape[:-2] + (1, shape[-1] // 4)) > 0.0625), 4, axis=-1).astype(np.float32)
    return mx_ref.flush(v.astype(BF))
C = 352
STEP = [1, 2, 4]
def numbers_of(rng):
    return {"x": np.array(f(rng, N, 128, 4 * C)), "u": np.array(f(rng, N, 128, 512)), "v": np.array(f(rng, N, 128, 512))}
def stored(a, b):
    return {"lam": np.stack([gtable(a[r]) for r in range(N)]), "rho": np.stack([gtable(b[r]) for r in range(N)])}
def dealt(rng):
    e = np.tile(np.arange(C), (N, 8, 1))
    return np.stack([rng.permuted(e, axis=2), rng.permuted(e, axis=2)], axis=3).reshape(N, 8, 2 * C)
def lists(rng):
    a = dealt(rng)
    return stored(a, dealt(rng))
def layers(rng):
    return np.array(f(rng, N, 128, 2048)).reshape(N, 8, 16, 4, 8, 16, 4)
def weights(rng, w):
    c, p = packed(np.ascontiguousarray(w).reshape(N, 128, 2048), rng)
    return {"wc": c, "ws": p}
def unread(u):
    u = u.reshape(N, 128, 128, 4)
    u[:, :, ::16] = 0
    u[:, :, 1::16] = 0
    return u
def setup_inputs(rng):
    return {**numbers_of(rng), **lists(rng), **weights(rng, layers(rng))}
def setup_inputs_ties(rng):
    d = numbers_of(rng)
    o = rng.permutation(N)
    s = rng.integers(-1, 2, (N, 8, 2, C)).astype(np.float32)
    s[o[1]] = 1
    s[o[2]] = -1
    x = d["x"].reshape(N, 8, 16, C, 4)
    x[:, :, :2] = 0
    x[:, :, :2, :, 0] = s.astype(BF)
    c = np.ones(N, np.float32)
    c[o[0]] = 0
    u = unread(d["u"])
    for h in range(0, 128, 16):
        for i in range(2): u[:, h + i, h + i, 0] = c.astype(BF)
    w = layers(rng)
    w[:, :, :, :, :, :8] = 0
    for g in range(8): w[:, g, 15, 0, g, 15, 0] = 2.0 ** 8
    return {"x": x.reshape(N, 128, 4 * C), "u": u.reshape(N, 128, 512), "v": d["v"], **lists(rng), **weights(rng, w)}
def setup_inputs_near(rng):
    d = numbers_of(rng)
    lo = np.unique(np.minimum(np.arange(N), np.arange(N) ^ STEP[0]))
    o = np.zeros(N, np.int64)
    o[lo] = rng.permutation(N // 2) % 2
    o[lo ^ STEP[0]] = o[lo]
    k = np.where(o == 0, 2.0 ** -30, 1.0).astype(np.float32)
    some = rng.permutation(8)[:4]
    x = d["x"].astype(np.float32).reshape(N, 8, 16, C, 4)
    x[:, :, :8] = 0
    x[:, some, 8:] = 0
    for g in some: x[:, g, 15, :, 0] = k[:, None]
    for i in range(2):
        s = rng.integers(-1, 2, (N, 8, C)) * k[:, None, None]
        x[:, :, 2 * i, :, 0] = 1.125 * s
        x[:, :, 2 * i + 1, :, 0] = -1.25 * s
        x[:, :, 6, :, i] = rng.choice([-1.0, 1.0], (N, 8, C)) * k[:, None, None]
        x[:, :, 6, :, 2 + i] = rng.choice([-1.0, 1.0], (N, 8, C)) * k[:, None, None]
    x[:, :, 7, :, 0] = k[:, None, None]
    for r in range(N):
        for g in rng.permutation(8)[:4]: x[r, g, 2 * rng.integers(2), rng.integers(C), 0] = 2.0 ** 30 * rng.choice([-1.0, 1.0])
    u = unread(d["u"])
    for h in range(0, 128, 16):
        for i in range(2):
            u[:, h + 2 * i, h + i, 0] = (1.125 * k).astype(BF)
            u[:, h + 2 * i + 1, h + i, 0] = k.astype(BF)
            u[:, h + 4 + i, h + i, 0] = k.astype(BF)
    w = layers(rng)
    w[:, :, :8] = 0
    w[:, :, :, :, :, :8] = 0
    w[:, :8] = 0
    for g in range(8):
        for i in range(2): w[:, g, 6, 0, g, 4 + i, i] = 2.0 ** -8
        w[:, g, 7, 0, g, 7, 0] = 32.0
    for g in some:
        for i in range(2):
            u[:, 16 * g + 8 + 2 * i, 16 * g + i, 0] = (1.125 * k).astype(BF)
            u[:, 16 * g + 9 + 2 * i, 16 * g + i, 0] = k.astype(BF)
            w[:, g, 6, 0, g, 8 + 2 * i, 2 + i] = 1.125 * 2.0 ** -8
            w[:, g, 6, 0, g, 9 + 2 * i, 2 + i] = -1.25 * 2.0 ** -8
        w[:, g, 7, 0, g, 14, 0] = 32.0
    return {"x": x.reshape(N, 128, 4 * C).astype(BF), "u": u.reshape(N, 128, 512), "v": d["v"], **lists(rng), **weights(rng, w)}
def setup_inputs_odd(rng):
    d = numbers_of(rng)
    x = d["x"].astype(np.float32).reshape(N, 8, 16, C, 4)
    x[:, :, 8:] = 0
    x[:, :, 0, :, 0] = 1.96875 * 2.0 ** 8
    for i in range(2):
        x[:, :, 1 + 2 * i, :, 0] = 2.0 ** -5
        x[:, :, 2 + 2 * i, :, 0] = (7 + 2 * rng.integers(0, 2, (N, 8, C))) * 2.0 ** -8
    x[:, :, 8, :, 0] = -1.125
    x[:, :, 10, :, 0] = 0.0703125 * rng.choice([-1.0, 1.0], (N, 8, C))
    u = unread(d["u"])
    for h in range(0, 128, 16):
        for i in range(2):
            c = rng.choice([-1.0, 1.0], N).astype(np.float32)
            u[:, h + 1 + 2 * i, h + i, 0] = c.astype(BF)
            u[:, h + 2 + 2 * i, h + i, 0] = (-1.125 * c).astype(BF)
    w = np.zeros((N, 8, 16, 4, 8, 16, 4), np.float32)
    for g in range(8):
        w[:, g, 8, 0, g, 8, 0] = -28.0
        w[:, g, 2, 0, g, 12, 0] = 32.0
        for b in range(4): w[:, g, 10, b, g, 9, 0] = -2.0 ** (b - 5)
    return {"x": x.reshape(N, 128, 4 * C).astype(BF), "u": u.reshape(N, 128, 512), "v": d["v"], **lists(rng), **weights(rng, w.astype(BF))}
def setup_inputs_ends(rng):
    d = numbers_of(rng)
    o, e = rng.permutation(N) % 4, rng.permutation(N) % 4
    s = rng.choice([-1.0, 1.0], (N, 128, C, 4))
    s[o == 0] = -1
    s[o == 1] = rng.choice([-1.0, 1.0], (N, 1, C, 1))[o == 1]
    x = s * (0.93 + 0.02 * rng.random((N, 128, C, 4))) * 2.0 ** 30
    x[o == 3] = 2.0 ** -30
    size = np.where(o == 3, 2.0 ** -30, 2.0 ** 30)
    u = unread(d["u"])
    for r in range(N):
        h = rng.permutation(8)
        for i in range(2):
            c = np.where(h < 2, 0.0, ((h >> i) % 2) * 2.0 - 1.0) * size[r]
            u[r, :, i::16] = c.astype(np.float32).astype(BF)[None, :, None]
    v = rng.choice([-1.0, 1.0], (N, 128, 512)) * np.where(o < 2, 2.0 ** 30, 2.0 ** -30)[:, None, None]
    t = rng.integers(0, C, (2, N, 8, 2 * C))
    t[:, e == 0] = C - 1
    t[:, e == 1] = 0
    t[:, e == 2] = np.arange(2 * C) % 2 * (C - 1)
    w = np.zeros((N, 128, 4, 128, 4), np.float32)
    j = np.arange(127)
    for b in range(4): w[:, j, b, j, b] = np.array([-0.25, -0.25, -2.0 ** -8, 32.0])[o][:, None]
    return {"x": x.astype(np.float32).reshape(N, 128, 4 * C).astype(BF), "u": u.reshape(N, 128, 512), "v": v.astype(np.float32).astype(BF), **stored(t[0], t[1]), **weights(rng, w.astype(BF))}
def setup_inputs_spread(rng):
    d = setup_inputs(rng)
    d["x"] = wide(rng, N, 128, 4 * C, cols=6)
    return d
def check_inputs(d):
    b = []
    for k in ("x", "u", "v"):
        a = np.abs(d[k].astype(np.float32))
        if not (np.isfinite(a).all() and ((a == 0) | (a >= 2.0 ** -30) & (a <= 2.0 ** 30)).all()): b.append("a value of " + k)
    for k in ("lam", "rho"):
        if not ((d[k] >= 0) & (d[k] < C)).all(): b.append("an entry of " + k)
    none, least, most = [emit(mx_ref.quantize(np.full((128, 16), k, np.float32).astype(BF)))[1][0, 0] for k in (0.0, 2.0 ** -8, 2.0 ** 8)]
    for r in range(N):
        if ((d["wc"][r] == 0x7F) | (d["wc"][r] == 0xFF)).any(): b.append("wc: a code that is no number")
        s = mx_ref.live(d["ws"][r])
        if ((s != none) & ((s < least) | (s > most))).any(): b.append("ws: a scale out of range")
        if (((d["wc"][r].reshape(16, 8, 512, 4) & 0x7F) != 0) & (s == none)[:, None, :, None]).any(): b.append("wc: a code other than zero under the scale of zeros")
    return b
def swapped(t, where):
    a = t.reshape(8, C, 2)
    return np.where(where[:, :, None], a[:, :, ::-1], a).reshape(8, 2 * C)
def reference(x, u, v, lam, rho, wc, ws):
    qu = [mx_ref.quantize(u[r]) for r in range(N)]
    lay = [pk(wc[r], ws[r]) for r in range(N)]
    left, right = [gentries(lam[r]) for r in range(N)], [gentries(rho[r]) for r in range(N)]
    now = [x[r] for r in range(N)]
    q = [mx_ref.quantize(now[r]) for r in range(N)]
    s = [mx_ref.matmul(qu[r], q[r]) for r in range(N)]
    for step in STEP:
        at, mid, sent = [], [], []
        for r in range(N):
            bit = (s[r][::16] > 0).astype(np.int64)
            up, down = np.zeros((8, C), np.int64), np.zeros((8, C), np.int64)
            up[0] = np.arange(C)
            down[7] = np.arange(C)
            for g in range(7):
                up[g + 1] = left[r][g][2 * up[g] + bit[g]]
            for g in range(7, 0, -1):
                down[g - 1] = right[r][g][2 * down[g] + bit[g]]
            at.append(np.take_along_axis(up, down, axis=1))
            mid.append(((now[r].astype(np.float32) + gcols(now[r], at[r]).astype(np.float32)) * np.float32(0.5)).astype(BF))
            z = mx_ref.quantize(mid[r])
            sent.append(mx_ref.quantize(tile([mx_ref.matmul(pick(lay[r], np.arange(128 * b, 128 * b + 128)), z) * np.float32(0.03125) for b in range(4)])))
        for r in range(N):
            p = r ^ step
            far = gcols(decode(sent[p]).astype(BF), np.take_along_axis(at[p], at[r], axis=1))
            now[r] = (mid[r].astype(np.float32) + far.astype(np.float32)).astype(BF)
            q[r] = mx_ref.quantize(now[r])
            s[r] = mx_ref.matmul(qu[r], q[r])
            left[r], right[r] = swapped(left[r], s[r][1::16] < 0), swapped(right[r], s[r][1::16] > 0)
    y, lr = np.zeros((N, 128, C), np.float32), np.zeros((N, 8, 4 * C), np.float32)
    oc, osc = np.zeros((N, 128, 4 * C), np.uint8), np.zeros((N, 16, C), np.uint8)
    for r in range(N):
        y[r] = mx_ref.matmul(mx_ref.quantize(v[r]), q[r])
        lr[r] = np.concatenate([left[r], right[r]], axis=1)
        oc[r], osc[r] = emit(q[r])
    return {"y": y, "lr": lr, "oc": oc, "osc": osc}

@@ -1,0 +1,360 @@
+from concourse.bass import DstId, RemoteDMATransfer
+from concourse.mybir import dt, AluOpType, ActivationFunctionType
+
+C = 352
+STEP = (1, 2, 4)
+CH = ((0, 192), (192, 352))
+PLACES = 1
+LATE = 3
+A = AluOpType
+COPY = ActivationFunctionType.Copy
+SIGN = ActivationFunctionType.Sign
+F8 = "float8_e4m3fn_x4"
+
+SCRATCH = {
+    "xt": ("sbuf", [128, 4 * C], "bfloat16"), "xh": ("sbuf", [128, 4 * C], "bfloat16"),
+    "vt": ("sbuf", [128, 4 * C], "bfloat16"), "hp": ("sbuf", [128, 4 * C], "bfloat16"),
+    "hl": ("sbuf", [128, 4 * C], "bfloat16"), "dp": ("sbuf", [128, 4 * C], "bfloat16"),
+    "ut": ("sbuf", [128, 512], "bfloat16"), "vv": ("sbuf", [128, 512], "bfloat16"), "et": ("sbuf", [128, 2048], "bfloat16"),
+    "one": ("sbuf", [128, 512], "bfloat16"), "xi": ("sbuf", [128, 4 * C], "bfloat16"),
+    "xq": ("sbuf", [128, C], F8), "xs": ("sbuf", [128, C], "uint8"),
+    "vq": ("sbuf", [128, C], F8), "vs": ("sbuf", [128, C], "uint8"),
+    "uq": ("sbuf", [128, 128], F8), "us": ("sbuf", [128, 128], "uint8"),
+    "pq": ("sbuf", [128, 256], F8), "ps": ("sbuf", [128, 256], "uint8"),
+    "zq": ("sbuf", [128, 128], F8), "zs": ("sbuf", [128, 128], "uint8"),
+    "eq": ("sbuf", [128, 512], F8), "es": ("sbuf", [128, 512], "uint8"),
+    "wq": ("sbuf", [128, 512], F8), "wp": ("sbuf", [128, 512], "uint8"),
+    "ti": ("sbuf", [128, 704], "int32"), "tf": ("sbuf", [128, 704], "float32"), "idt": ("sbuf", [128, 704], "int32"),
+    "d0": ("sbuf", [128, 1056], "float32"), "d1": ("sbuf", [128, 1056], "float32"), "tw": ("sbuf", [128, 1056], "float32"),
+    "sb": ("sbuf", [128, C], "float32"), "bra": ("sbuf", [128, 128], "float32"), "brb": ("sbuf", [128, 128], "float32"),
+    "gm": ("sbuf", [128, 128], "float16"), "zm": ("sbuf", [128, 128], "float16"), "g0": ("sbuf", [128, 128], "float32"), "g2": ("sbuf", [128, 128], "float32"),
+    "g4": ("sbuf", [128, 128], "float32"), "g6": ("sbuf", [128, 128], "float32"), "zt": ("sbuf", [128, 128], "float32"),
+    "off": ("sbuf", [128, 8], "uint16"), "sl": ("sbuf", [128, 16], "uint16"), "ul": ("sbuf", [128, 16], "uint16"),
+    "lw": ("sbuf", [128, 768], "float32"), "rl": ("sbuf", [128, 32], "float32"), "ri": ("sbuf", [128, 32], "int32"),
+    "ro": ("sbuf", [128, 22], "uint16"), "gcm": ("sbuf", [128, C], "float16"), "zc": ("sbuf", [128, C], "float16"),
+    "ko": ("sbuf", [128, 22], "uint16"), "yw": ("sbuf", [128, C], "float32"), "roe": ("sbuf", [128, 22], "uint16"), "eo": ("sbuf", [128, 22], "uint16"),
+    "lk": ("sbuf", [128, 704], "int32"),
+    "ci": ("sbuf", [128, 16], "int32"), "cf": ("sbuf", [128, 16], "float32"), "fw": ("sbuf", [128, 16], "float32"),
+    "fc": ("sbuf", [128, 128], "float32"), "c3": ("sbuf", [128, 128], "float32"), "z8": ("sbuf", [128, 8], "float32"),
+    "yt": ("sbuf", [128, C], "float32"), "lt": ("sbuf", [128, 704], "float32"),
+    "pm": ("psum", [128, 4096], "float32"),
+}
+for _r in range(3):
+    SCRATCH["hq%d" % _r] = ("sbuf", [128, C], F8)
+    SCRATCH["hs%d" % _r] = ("sbuf", [128, C], "uint8")
+    SCRATCH["aq%d" % _r] = ("sbuf", [128, C], F8)
+    SCRATCH["as%d" % _r] = ("sbuf", [128, C], "uint8")
+    SCRATCH["ki%d" % _r] = ("sbuf", [128, 22], "int32")
+    SCRATCH["ka%d" % _r] = ("sbuf", [128, 22], "int32")
+SEMAPHORES = (["sv", "ss", "st", "sg", "lu", "lx", "lt", "lid", "lw", "lv", "snt", "outs"]
+              + [n % r for r in range(3) for n in ("hop%d", "kop%d", "ark%d")] + ["arr%d%d" % (r, c) for r in range(3) for c in range(2)])
+
+
+def rank_program(g, core, T, topo):
+    rank = T.rank_of(core)
+    if rank is None:
+        return
+    Q = {"v": g.vector, "s": g.scalar, "t": g.tensor, "g": g, "y": g.sync}
+    SEM = {"v": "sv", "s": "ss", "t": "st", "g": "sg"}
+    total = {}
+    waited = {}
+    gens = {}
+
+    def need(qn, toks):
+        best = {}
+        for s, n in toks:
+            n = total[s] if n is None else n
+            best[s] = max(best.get(s, 0), n)
+        for s, n in best.items():
+            if waited.get((qn, s), 0) < n:
+                Q[qn].wait_ge(T.sem[s], n)
+                waited[(qn, s)] = n
+
+    def before(qn, R, W):
+        toks = []
+        for k in R:
+            toks += gens.setdefault(k, [[], [], []])[1]
+        for k in W:
+            e = gens.setdefault(k, [[], [], []])
+            if e[2]:
+                gens[k] = e = [e[1] + e[2], [], []]
+            toks += e[0]
+        need(qn, toks)
+
+    def after(tok, R, W):
+        for k in R:
+            gens[k][2].append(tok)
+        for k in W:
+            gens[k][1].append(tok)
+
+    def op(qn, fn, args, R, W, kw=None):
+        before(qn, R, W)
+        s = SEM[qn]
+        fn(*args, **(kw or {})).then_inc(T.sem[s], 1)
+        total[s] = total.get(s, 0) + 1
+        after((s, total[s]), R, W)
+
+    def dma(qn, out, in_, R, W, sem):
+        before(qn, R, W)
+        Q[qn].dma_start(out, in_).then_inc(T.sem[sem], 16)
+        total[sem] = total.get(sem, 0) + 16
+        after((sem, None), R, W)
+
+    V, S, TE = g.vector, g.scalar, g.tensor
+
+    def ts(out, in0, s1, s2, o0, o1, R, W):
+        if o1 is None:
+            op("v", V.tensor_scalar, (out, in0, s1, None, o0), R, W)
+        else:
+            op("v", V.tensor_scalar, (out, in0, s1, s2, o0, o1), R, W)
+
+    def tt(out, a, b, o, R, W):
+        op("v", V.tensor_tensor, (out, a, b, o), R, W)
+
+    def tc(out, a, R, W):
+        op("v", V.tensor_copy, (out, a), R, W)
+
+    def act(out, a, R, W, **kw):
+        op("s", S.activation, (out, a, COPY), R, W, kw)
+
+    def bank(i, n=C):
+        return T.pm[:, 512 * i:512 * i + n]
+
+    def mm(i, n, lq, ls, rq, rs, R):
+        op("t", TE.matmul_mx, (bank(i, n), lq, ls, rq, rs, True, True), R, ["b%d" % i])
+
+    def quant(q, s, t, R, W):
+        op("v", V.quantize_mx, (q, s, t), R, W)
+
+    def u8(v):
+        return v.bitcast(dt.uint8)
+
+    dma("s", T.ut[:], T.u[:], [], ["ut"], "lu")
+    dma("y", T.xt[:], T.x[:], [], ["xt"], "lx")
+    for h in range(8):
+        qn = "y" if h % 2 else "s"
+        if h == 1:
+            dma(qn, T.ti[16:23, :], T.lam[0:112, :], [], ["ti"], "lt")
+            dma(qn, T.ti[23:24, :], T.rho[0:16, :], [], ["ti"], "lt")
+        else:
+            dma(qn, T.ti[16 * h:16 * h + 8, :], T.lam[:], [], ["ti"], "lt")
+        dma(qn, T.ti[16 * h + 9:16 * h + 16, :], T.rho[16:128, :], [], ["ti"], "lt")
+    dma("s", u8(T.wq[:, :]), T.wc[:], [], ["wq"], "lw")
+    dma("s", T.wp[:], T.ws[:], [], ["wq"], "lw")
+    dma("s", T.vv[:], T.v[:], [], ["vv"], "lv")
+
+    def iota(out, pat, base, cm, W, f=True):
+        kw = {"allow_small_or_imprecise_dtypes": True} if f else {}
+        op("g", g.iota, (out, pat, base, cm), [], W, kw)
+    iota(T.ci[:, 0:1], [[0, 1]], 0, 1, ["ci0"], False)
+    iota(T.idt[:, :], [[1, 8], [0, 2], [8, 44]], 0, 0, ["idt"], False)
+    dma("y", T.ti[8:128:16, :], T.idt[0:8, :], ["idt"], ["ti"], "lt")
+    iota(T.fw[:, 0:4], [[16, 4]], 0, 0, ["fw"])
+    iota(T.fw[:, 4:8], [[1, 4]], 0, 0, ["fw"])
+    iota(T.fw[:, 8:12], [[32, 2], [48, 2]], 0, 0, ["fw"])
+    iota(T.fw[:, 12:16], [[2, 2], [4, 2]], 0, 0, ["fw"])
+    iota(T.fc[:, 0:64], [[32, 2], [48, 2], [1, 16]], 0, 0, ["fc"])
+    iota(T.fc[:, 64:128], [[2, 2], [4, 2], [32, 16]], 0, 0, ["fc"])
+    op("v", V.memset, (T.z8[:], 0.0), [], ["z8"])
+
+    def I(k):
+        return T.ci[:, k:k + 1]
+
+    def F(k):
+        return T.cf[:, k:k + 1]
+    SR, AND = A.logical_shift_right, A.bitwise_and
+    ts(I(1), I(0), 15, None, AND, None, ["ci0"], ["ci1"])
+    ts(I(2), I(0), 3, 1, SR, AND, ["ci0"], ["ci2"])
+    ts(I(3), I(0), 7, None, AND, None, ["ci0"], ["ci3"])
+    ts(I(4), I(0), 4, None, SR, None, ["ci0"], ["ci4"])
+    ts(I(5), I(0), 5, None, SR, None, ["ci0"], ["ci5"])
+    ts(I(6), I(0), 4, 1, SR, AND, ["ci0"], ["ci6"])
+    ts(I(7), I(2), -2, 1, A.mult, A.add, ["ci2"], ["ci7"])
+    tt(I(8), I(7), I(1), A.add, ["ci7", "ci1"], ["ci8"])
+    ts(I(9), I(8), 7, None, AND, None, ["ci8"], ["ci9"])
+    ts(F(0), I(9), 16.0, None, A.mult, None, ["ci9"], ["f0"])
+    ts(F(1), I(3), 16.0, 1.0, A.mult, A.add, ["ci3"], ["f1"])
+    ts(F(2), I(1), 7.0, -112.0, A.is_equal, A.mult, ["ci1"], ["f2"])
+    ts(T.ul[:, 0:8], T.z8[:], F(0), None, A.add, None, ["z8", "f0"], ["ul"])
+    ts(T.ul[:, 8:16], T.z8[:], F(1), None, A.add, None, ["z8", "f1"], ["ul"])
+    need("v", [("sv", total["sv"])])
+    ts(T.ul[:, 9:10], F(2), F(1), None, A.add, None, ["f1", "f2"], ["ul"])
+    ts(F(3), I(7), 1.0, None, A.mult, None, ["ci7"], ["f3"])
+    ts(F(4), I(0), 23.0, -2.0, A.is_equal, A.mult, ["ci0"], ["f4"])
+    tt(F(5), F(3), F(4), A.add, ["f3", "f4"], ["f5"])
+    tc(F(6), I(1), ["ci1"], ["f6"])
+    ts(F(7), I(1), 32.0, None, A.mult, None, ["ci1"], ["f7"])
+    tc(F(8), I(6), ["ci6"], ["f8"])
+    ts(F(9), I(4), 48.0, F(6), A.mult, A.add, ["ci4", "f6"], ["f9"])
+    ts(F(10), I(4), 4.0, F(7), A.mult, A.add, ["ci4", "f7"], ["f10"])
+    ts(F(11), I(6), 16.0, None, A.mult, None, ["ci6"], ["f11"])
+    ts(F(12), I(5), 96.0, F(11), A.mult, A.add, ["ci5", "f11"], ["f12"])
+    ts(F(13), I(5), 8.0, F(8), A.mult, A.add, ["ci5", "f8"], ["f13"])
+    tt(F(14), F(12), F(6), A.add, ["f12", "f6"], ["f14"])
+    tt(F(15), F(13), F(7), A.add, ["f13", "f7"], ["f15"])
+    for k, f in ((0, 9), (4, 10), (8, 14), (12, 15)):
+        ts(T.sl[:, k:k + 4], T.fw[:, k:k + 4], F(f), 351.0, A.add, A.min, ["fw", "f%d" % f], ["sl"])
+    ts(T.fc[:, 0:64], T.fc[:, 0:64], F(12), 351.0, A.add, A.min, ["fc", "f12"], ["fca"])
+    ts(T.fc[:, 64:128], T.fc[:, 64:128], F(13), 351.0, A.add, A.min, ["fc", "f13"], ["fca"])
+    ts(T.c3[:], T.fc[:], 3.0, None, A.mult, None, ["fca"], ["c3"])
+    ts(F(4), I(6), 352.0, None, A.mult, None, ["ci6", "f4", "f5"], ["hof"])
+    for k, val in ((0, 0), (1, 1), (2, -1)):
+        iota(T.d0[:, k:1056:3], [[0, C]], val, 0, ["phi" if k == 1 else "d0c"])
+    quant(T.uq[:], T.us[:], T.ut[:], ["ut"], ["uq"])
+    op("v", V.tensor_copy, (T.pq[:, 0:256].bitcast(dt.uint32), T.uq[:, 0:128].bitcast(dt.uint32).indirect(T.ul[:, 0:16])), ["uq", "ul"], ["pq"])
+    act(T.ps[:, 0:256], T.us[:, 0:128].indirect(T.ul[:, 0:16]), ["uq", "ul"], ["pq"])
+    quant(T.xq[:], T.xs[:], T.xt[:], ["xt"], ["xq"])
+
+    def scores(rows):
+        for k in rows:
+            mm(k, C, T.pq[:, 128 * k:128 * k + 128], T.ps[:, 128 * k:128 * k + 128], T.xq[:], T.xs[:], ["pq", "xq"])
+    scores([0])
+    for r in range(8):
+        e, o = T.ti[:, 88 * r:88 * r + 44], T.ti[:, 88 * r + 44:88 * r + 88]
+        tt(T.d1[:, 3 * r + 1:1056:24], o, e, A.add, ["ti"], ["d1s"])
+    for r in range(8):
+        e, o = T.ti[:, 88 * r:88 * r + 44], T.ti[:, 88 * r + 44:88 * r + 88]
+        tt(T.d1[:, 3 * r:1056:24], o, e, A.subtract, ["ti"], ["d1d"])
+    act(T.d1[:, 2:1056:3], T.d1[:, 1:1056:3], ["d1s"], ["d1n"], scale=3.0)
+    act(T.d1[:, 1:1056:3], T.d1[:, 1:1056:3], ["d1s"], ["d1m"], scale=1.5)
+    act(T.d1[:, 0:1056:3], T.d1[:, 0:1056:3], ["d1d"], ["d1b"], scale=1.5)
+    iota(T.rl[:, :], [[0, 2], [96, 16]], -287, 3, ["rli"])
+    iota(T.lw[:, :], [[3, 768]], 1, 0, ["lwz"])
+    iota(T.one[:, :], [[0, 512]], 1, 0, ["one"])
+    for b in range(4):
+        op("g", g.affine_select, (T.et[:, 512 * b:512 * b + 512], T.one[:], [[-1, 512]], A.is_equal, 0.0, b, 4), ["one"], ["et"])
+
+    iota(T.yw[:, :], [[1, 22], [22, 16]], 0, 0, ["yw0"])
+    iota(T.lk[:, :], [[0, 704]], 0, 0, ["lkz"], False)
+    K12 = (T.ko[:, 0:CH[0][1] // 16], T.ko[:, CH[0][1] // 16:22])
+
+    def plane(t, b, c0=0, c1=C):
+        return t[:, C * b + c0:C * b + c1]
+
+    def inter(t, b, c0=0, c1=C):
+        return t[:, 4 * c0 + b:4 * c1:4]
+
+    for rnd in range(3):
+        partner = T.cores[rank ^ STEP[rnd]]
+        if rnd:
+            op("s", S.activation, (T.d0[:, 1:1056:3], bank(1), SIGN), ["b1", "f5"], ["phi"], {"bias": 2.0 ** -94, "scale": F(5)})
+        ts(T.sb[:], bank(0), 0.0, 1.0, A.is_le, A.add, ["b0"], ["sb"])
+        tt(T.gm[:], T.sb[:].indirect(T.sl[:, 8:16]), T.c3[:], A.add, ["sb", "sl", "c3"], ["gm"])
+
+        def wrap(src, key, ql, qr):
+            z = "zm" if key == "gm" else "zt"
+            op("v", V.transpose, (T[z][:], src), [key], [z])
+            tc(T.off[:, 0:4], T[z][:, ql:64:16], [z], ["off"])
+            tc(T.off[:, 4:8], T[z][:, 64 + qr:128:16], [z], ["off"])
+        wrap(T.gm[:], "gm", 7, 8)
+        act(T.bra[:], T.sb[:].indirect(T.sl[:, 0:8]), ["sb", "sl"], ["bra"])
+        act(T.brb[:], T.sb[:].indirect(T.sl[:, 8:16]), ["sb", "sl"], ["brb"])
+        for b in range(4):
+            act(plane(T.xh, b), inter(T.xt, b), ["xt"], ["xh%d" % b], scale=0.5)
+        act(T.xi[:], T.xt[:], ["xt"], ["xi"], scale=0.5)
+        op("v", V.tensor_tensor_scan, (T.tw[:], T.d0[:], T.d1[:], 0.0, A.mult, A.add), ["d0c", "phi", "d1b", "d1m", "d1n"], ["tw"])
+        hop = "hop%d" % rnd
+
+        def land(qn, gt, key, lists):
+            for kind, q, to in lists:
+                a, h = to // 2, to % 2
+                if kind == "l":
+                    for d in (0, 16):
+                        dma(qn[0], T.lw[32 * a + d:32 * a + d + 1, 384 * h:384 * h + 384], gt[q:128:16, 0:48], [key, "lwz"], ["lw"], hop)
+                        qn = qn[1:] + qn[:1]
+                else:
+                    dma(qn[0], T.rl[32 * a:32 * a + 32, 16 * h:16 * h + 16], gt[q:128:16, 64:128], [key, "rli"], ["rl"], hop)
+                    qn = qn[1:] + qn[:1]
+        for t in range(7):
+            name = "gm" if t % 2 else "g%d" % t
+            tt(T[name][:], T.tw[:].indirect(T.off[:, 0:8]), (T.brb if t % 2 else T.bra)[:], A.add, ["tw", "off", "brb" if t % 2 else "bra"], [name])
+            if t < 6:
+                wrap(T[name][:], name, t, 15 - t)
+            if t % 2 == 0:
+                todo = [("l", t, t + 1), ("r", 15 - t, 6 - t)]
+                if t:
+                    todo += [("l", 8, t), ("r", 8, 7 - t)]
+                land("y" if t < 6 else "ys", T[name], name, todo)
+        if rnd:
+            tt(T.d1[:, 0:1056:3], T.d1[:, 0:1056:3], T.d0[:, 1:1056:3], A.mult, ["d1b", "phi"], ["d1b"])
+        else:
+            quant(T.eq[:], T.es[:], T.et[:], ["et"], ["eq"])
+        if rnd == 2:
+            quant(T.zq[:], T.zs[:], T.vv[:], ["vv"], ["zq"])
+        if rnd == 0:
+            ts(T.yw[:], T.yw[:], F(4), None, A.add, None, ["yw0", "hof"], ["yw"])
+        for h in range(2):
+            ts(T.ro[:, h:22:2], T.rl[:, 16 * h:16 * h + 11], 1152.0 * h - 1.0, 1.0 / 3.0, A.add, A.mult, ["rl", "rli"], ["ro"])
+        tc(T.gcm[:], T.lw[:].indirect(T.ro[:]), ["lw", "lwz", "ro"], ["gcm"])
+        op("v", V.transpose, (T.zc[:], T.gcm[:]), ["gcm"], ["zc"])
+        ki, kk = T["ki%d" % rnd], "ki%d" % rnd
+        ts(ki[:], T.zc[:, 0:352:16], -1.0, 1.0 / 3.0, A.add, A.mult, ["zc"], [kk])
+        ts(T.ko[:], T.zc[:, 0:352:16], -1.0, 1.0 / 3.0, A.add, A.mult, ["zc"], ["ko"])
+        rid, pid = topo.addr(partner)[0:2]
+        mask = topo.mask(core, partner)
+        ne = len(topo.engines(core, partner))
+        hq, hs, aq, as_ = T["hq%d" % rnd], T["hs%d" % rnd], T["aq%d" % rnd], T["as%d" % rnd]
+
+        def send(out, in_, sem, key):
+            before("g", [key], [])
+            g.remote_dma(out, in_, T.sem[sem], T.sem.snt, pid, rid, mask)
+            total["snt"] = total.get("snt", 0) + ne
+            total[sem] = total.get(sem, 0) + ne
+
+        def send_h(c):
+            c0, c1 = CH[c]
+            quant(hq[:, c0:c1], hs[:, c0:c1], T.hl[:, 4 * c0:4 * c1], ["hl%d" % c], ["hq%d%d" % (rnd, c)])
+            send(u8(aq[:, c0:c1]), u8(hq[:, c0:c1]), "arr%d%d" % (rnd, c), "hq%d%d" % (rnd, c))
+            send(as_[:, c0:c1], hs[:, c0:c1], "arr%d%d" % (rnd, c), "hq%d%d" % (rnd, c))
+        send(T["ka%d" % rnd][:], ki[:], "ark%d" % rnd, kk)
+        for c, (c0, c1) in enumerate(CH):
+            for b in range(4):
+                if c == 1 and b == LATE:
+                    send_h(0)
+                tt(inter(T.vt, b, c0, c1), plane(T.xh, b).indirect(K12[c]), inter(T.xi, b, c0, c1), A.add, ["xh%d" % b, "xi", "ko"], ["vt%d" % c])
+            quant(T.vq[:, c0:c1], T.vs[:, c0:c1], T.vt[:, 4 * c0:4 * c1], ["vt%d" % c], ["vq%d" % c])
+            for b in range(4):
+                mm(4 * c + b, c1 - c0, T.wq[:, 128 * b:128 * b + 128], T.wp[:, 128 * b:128 * b + 128], T.vq[:, c0:c1], T.vs[:, c0:c1], ["wq", "vq%d" % c])
+                if c == 0 or b % 2:
+                    act(inter(T.hl, b, c0, c1), bank(4 * c + b, c1 - c0), ["b%d" % (4 * c + b)], ["hl%d" % c], scale=0.03125)
+            if c == PLACES:
+                tc(T.gcm[:], T.yw[:].indirect(T.ko[:]), ["yw", "ko"], ["gcm"])
+            if c == 1:
+                for b in (0, 2):
+                    ts(inter(T.hl, b, c0, c1), bank(4 + b, c1 - c0), 0.03125, None, A.mult, None, ["b%d" % (4 + b)], ["hl1"])
+                send_h(1)
+        for d in (0, 16):
+            need("y", [("ark%d" % rnd, None)])
+            dma("y", T.lk[d:128:32, :], T["ka%d" % rnd][:], ["lkz"], ["lk"], "kop%d" % rnd)
+        op("v", V.transpose, (T.zc[:], T.gcm[:]), ["gcm"], ["zc"])
+        tc(T.roe[:], T.zc[:, 0:352:16], ["zc"], ["roe"])
+        tc(T.gcm[:], T.lk[:].indirect(T.roe[:]), ["lk", "lkz", "roe"], ["gcm"])
+        op("v", V.transpose, (T.zc[:], T.gcm[:]), ["gcm"], ["zc"])
+        tc(T.eo[:], T.zc[:, 0:352:16], ["zc"], ["eo"])
+        for c, (c0, c1) in enumerate(CH):
+            need("t", [("arr%d%d" % (rnd, c), None)])
+            for b in range(4):
+                mm(4 * c + b, c1 - c0, T.eq[:, 128 * b:128 * b + 128], T.es[:, 128 * b:128 * b + 128], aq[:, c0:c1], as_[:, c0:c1], ["eq"])
+                if c == 0 or b % 2:
+                    act(plane(T.dp, b, c0, c1), bank(4 * c + b, c1 - c0), ["b%d" % (4 * c + b)], ["dp%d" % b])
+                else:
+                    tc(plane(T.dp, b, c0, c1), bank(4 * c + b, c1 - c0), ["b%d" % (4 * c + b)], ["dp%d" % b])
+        for b in (0, 2, 1, 3):
+            tt(inter(T.xt, b), plane(T.dp, b).indirect(T.eo[:]), inter(T.vt, b), A.add, ["dp%d" % b, "eo", "vt0", "vt1"], ["xt"])
+        quant(T.xq[:], T.xs[:], T.xt[:], ["xt"], ["xq"])
+        scores([0, 1] if rnd < 2 else [1])
+
+    mm(2, C, T.zq[:], T.zs[:], T.xq[:], T.xs[:], ["zq", "xq"])
+    dma("y", T.oc[:], u8(T.xq[:, :]), ["xq"], [], "outs")
+    for k in range(4):
+        dma("y", T.osc[4 * k:4 * k + 4, :], T.xs[32 * k:32 * k + 4, :], ["xq"], [], "outs")
+    op("s", S.activation, (T.d0[:, 1:1056:3], bank(1), SIGN), ["b1", "f5"], ["phi"], {"bias": 2.0 ** -94, "scale": F(5)})
+    tc(T.yt[:], bank(2), ["b2"], ["yt"])
+    dma("y", T.y[:], T.yt[:], ["yt"], [], "outs")
+    op("v", V.tensor_tensor_scan, (T.tw[:], T.d0[:], T.d1[:], 0.0, A.mult, A.add), ["d0c", "phi", "d1b", "d1m", "d1n"], ["tw"])
+    ts(T.lt[:, 0:704:2], T.tw[:, 2:1056:3], 1.0 / 3.0, None, A.mult, None, ["tw"], ["lt"])
+    act(T.lt[:, 1:704:2], T.tw[:, 1:1056:3], ["tw"], ["lt"], scale=1.0 / 3.0)
+    dma("y", T.lr[0:8, 0:704], T.lt[0:8, :], ["lt"], [], "outs")
+    dma("s", T.lr[1:8, 704:1408], T.lt[9:16, :], ["lt"], [], "outs")
+    dma("s", T.lr[0:1, 704:1408], T.lt[23:24, :], ["lt"], [], "outs")
+    need("g", [(s, None) for s in total if not s.startswith("ar")])

@@ -3,39 +3,43 @@ from concourse.mybir import dt, AluOpType, ActivationFunctionType
 
 C = 352
 STEP = (1, 2, 4)
-CH = ((0, 192), (192, 352))
-PLACES = 1
+CH = ((0, 224), (224, 352))
+XC = ((0, 192), (192, 352))
 LATE = 3
+MID = 176
+GAP = 0.2
 A = AluOpType
 COPY = ActivationFunctionType.Copy
+IDENT = ActivationFunctionType.Identity
 SIGN = ActivationFunctionType.Sign
 F8 = "float8_e4m3fn_x4"
 
 SCRATCH = {
-    "xt": ("sbuf", [128, 4 * C], "bfloat16"), "xh": ("sbuf", [128, 4 * C], "bfloat16"),
-    "vt": ("sbuf", [128, 4 * C], "bfloat16"), "hp": ("sbuf", [128, 4 * C], "bfloat16"),
-    "hl": ("sbuf", [128, 4 * C], "bfloat16"), "dp": ("sbuf", [128, 4 * C], "bfloat16"),
+    "xt": ("sbuf", [128, 4 * C], "bfloat16"), "xh": ("sbuf", [128, 4 * C], "bfloat16"), "xi": ("sbuf", [128, 4 * C], "bfloat16"),
+    "vt": ("sbuf", [128, 4 * C], "bfloat16"), "hl": ("sbuf", [128, 4 * C], "bfloat16"), "dp": ("sbuf", [128, 4 * C], "bfloat16"),
     "ut": ("sbuf", [128, 512], "bfloat16"), "vv": ("sbuf", [128, 512], "bfloat16"), "et": ("sbuf", [128, 2048], "bfloat16"),
-    "one": ("sbuf", [128, 512], "bfloat16"), "xi": ("sbuf", [128, 4 * C], "bfloat16"),
+    "one": ("sbuf", [128, 512], "bfloat16"), "eye": ("sbuf", [128, 128], "bfloat16"),
     "xq": ("sbuf", [128, C], F8), "xs": ("sbuf", [128, C], "uint8"),
     "vq": ("sbuf", [128, C], F8), "vs": ("sbuf", [128, C], "uint8"),
     "uq": ("sbuf", [128, 128], F8), "us": ("sbuf", [128, 128], "uint8"),
-    "pq": ("sbuf", [128, 256], F8), "ps": ("sbuf", [128, 256], "uint8"),
+    "pq": ("sbuf", [128, 384], F8), "ps": ("sbuf", [128, 384], "uint8"),
     "zq": ("sbuf", [128, 128], F8), "zs": ("sbuf", [128, 128], "uint8"),
     "eq": ("sbuf", [128, 512], F8), "es": ("sbuf", [128, 512], "uint8"),
     "wq": ("sbuf", [128, 512], F8), "wp": ("sbuf", [128, 512], "uint8"),
-    "ti": ("sbuf", [128, 704], "int32"), "tf": ("sbuf", [128, 704], "float32"), "idt": ("sbuf", [128, 704], "int32"),
+    "ti": ("sbuf", [128, 704], "int32"), "idt": ("sbuf", [128, 44], "int32"),
     "d0": ("sbuf", [128, 1056], "float32"), "d1": ("sbuf", [128, 1056], "float32"), "tw": ("sbuf", [128, 1056], "float32"),
-    "sb": ("sbuf", [128, C], "float32"), "bra": ("sbuf", [128, 128], "float32"), "brb": ("sbuf", [128, 128], "float32"),
-    "gm": ("sbuf", [128, 128], "float16"), "zm": ("sbuf", [128, 128], "float16"), "g0": ("sbuf", [128, 128], "float32"), "g2": ("sbuf", [128, 128], "float32"),
-    "g4": ("sbuf", [128, 128], "float32"), "g6": ("sbuf", [128, 128], "float32"), "zt": ("sbuf", [128, 128], "float32"),
-    "off": ("sbuf", [128, 8], "uint16"), "sl": ("sbuf", [128, 16], "uint16"), "ul": ("sbuf", [128, 16], "uint16"),
-    "lw": ("sbuf", [128, 768], "float32"), "rl": ("sbuf", [128, 32], "float32"), "ri": ("sbuf", [128, 32], "int32"),
-    "ro": ("sbuf", [128, 22], "uint16"), "gcm": ("sbuf", [128, C], "float16"), "zc": ("sbuf", [128, C], "float16"),
-    "ko": ("sbuf", [128, 22], "uint16"), "yw": ("sbuf", [128, C], "float32"), "roe": ("sbuf", [128, 22], "uint16"), "eo": ("sbuf", [128, 22], "uint16"),
-    "lk": ("sbuf", [128, 704], "int32"),
-    "ci": ("sbuf", [128, 16], "int32"), "cf": ("sbuf", [128, 16], "float32"), "fw": ("sbuf", [128, 16], "float32"),
-    "fc": ("sbuf", [128, 128], "float32"), "c3": ("sbuf", [128, 128], "float32"), "z8": ("sbuf", [128, 8], "float32"),
+    "sm": ("sbuf", [128, C], "float32"), "sb": ("sbuf", [128, C], "float32"),
+    "bra": ("sbuf", [128, 96], "float32"), "brb": ("sbuf", [128, 96], "float32"), "c3": ("sbuf", [128, 96], "float32"),
+    "gm": ("sbuf", [128, 192], "float32"), "g1": ("sbuf", [128, 96], "float32"), "g3": ("sbuf", [128, 96], "float32"), "g5": ("sbuf", [128, 96], "float32"),
+    "zm": ("sbuf", [128, 192], "float32"),
+    "off": ("sbuf", [128, 16], "uint16"), "mp": ("sbuf", [128, 18], "uint16"), "ul": ("sbuf", [128, 24], "uint16"),
+    "sel": ("sbuf", [128, 16], "uint16"), "fin": ("sbuf", [128, 2], "uint16"),
+    "lw": ("sbuf", [128, 768], "float32"), "ro": ("sbuf", [128, 22], "uint16"),
+    "gb": ("sbuf", [128, C], "bfloat16"), "zb": ("sbuf", [128, 384], "bfloat16"), "gh": ("sbuf", [128, C], "float16"), "zh": ("sbuf", [128, C], "float16"),
+    "ge": ("sbuf", [128, C], "bfloat16"), "ze": ("sbuf", [128, C], "bfloat16"),
+    "ko": ("sbuf", [128, 32], "uint16"), "yw": ("sbuf", [128, C], "float32"), "roe": ("sbuf", [128, 22], "uint16"), "eo": ("sbuf", [128, 22], "uint16"),
+    "lk": ("sbuf", [128, 704], "bfloat16"),
+    "ci": ("sbuf", [128, 48], "int32"), "cf": ("sbuf", [128, 48], "float32"), "gr": ("sbuf", [128, 32], "float32"), "fw": ("sbuf", [128, 32], "float32"),
     "yt": ("sbuf", [128, C], "float32"), "lt": ("sbuf", [128, 704], "float32"),
     "pm": ("psum", [128, 4096], "float32"),
 }
@@ -44,9 +48,9 @@ for _r in range(3):
     SCRATCH["hs%d" % _r] = ("sbuf", [128, C], "uint8")
     SCRATCH["aq%d" % _r] = ("sbuf", [128, C], F8)
     SCRATCH["as%d" % _r] = ("sbuf", [128, C], "uint8")
-    SCRATCH["ki%d" % _r] = ("sbuf", [128, 22], "int32")
-    SCRATCH["ka%d" % _r] = ("sbuf", [128, 22], "int32")
-SEMAPHORES = (["sv", "ss", "st", "sg", "lu", "lx", "lt", "lid", "lw", "lv", "snt", "outs"]
+    SCRATCH["ki%d" % _r] = ("sbuf", [128, 32], "bfloat16")
+    SCRATCH["ka%d" % _r] = ("sbuf", [128, 22], "bfloat16")
+SEMAPHORES = (["sv", "ss", "st", "sg", "lu", "lx0", "lx1", "lt", "lw", "lv", "snt", "outs"]
               + [n % r for r in range(3) for n in ("hop%d", "kop%d", "ark%d")] + ["arr%d%d" % (r, c) for r in range(3) for c in range(2)])
 
 
@@ -70,7 +74,7 @@ def rank_program(g, core, T, topo):
                 Q[qn].wait_ge(T.sem[s], n)
                 waited[(qn, s)] = n
 
-    def before(qn, R, W):
+    def before(qn, R, W, own=None):
         toks = []
         for k in R:
             toks += gens.setdefault(k, [[], [], []])[1]
@@ -78,7 +82,7 @@ def rank_program(g, core, T, topo):
             e = gens.setdefault(k, [[], [], []])
             if e[2]:
                 gens[k] = e = [e[1] + e[2], [], []]
-            toks += e[0]
+            toks += [t for t in e[0] if t[0] != own]
         need(qn, toks)
 
     def after(tok, R, W):
@@ -88,8 +92,8 @@ def rank_program(g, core, T, topo):
             gens[k][1].append(tok)
 
     def op(qn, fn, args, R, W, kw=None):
-        before(qn, R, W)
         s = SEM[qn]
+        before(qn, R, W, s)
         fn(*args, **(kw or {})).then_inc(T.sem[s], 1)
         total[s] = total.get(s, 0) + 1
         after((s, total[s]), R, W)
@@ -114,10 +118,13 @@ def rank_program(g, core, T, topo):
     def tc(out, a, R, W):
         op("v", V.tensor_copy, (out, a), R, W)
 
-    def act(out, a, R, W, **kw):
-        op("s", S.activation, (out, a, COPY), R, W, kw)
+    def turn(out, a, R, W):
+        op("v", V.transpose, (out, a), R, W)
 
-    def bank(i, n=C):
+    def act(out, a, R, W, fn=COPY, **kw):
+        op("s", S.activation, (out, a, fn), R, W, kw)
+
+    def bank(i, n):
         return T.pm[:, 512 * i:512 * i + n]
 
     def mm(i, n, lq, ls, rq, rs, R):
@@ -129,104 +136,172 @@ def rank_program(g, core, T, topo):
     def u8(v):
         return v.bitcast(dt.uint8)
 
-    dma("s", T.ut[:], T.u[:], [], ["ut"], "lu")
-    dma("y", T.xt[:], T.x[:], [], ["xt"], "lx")
-    for h in range(8):
-        qn = "y" if h % 2 else "s"
-        if h == 1:
-            dma(qn, T.ti[16:23, :], T.lam[0:112, :], [], ["ti"], "lt")
-            dma(qn, T.ti[23:24, :], T.rho[0:16, :], [], ["ti"], "lt")
-        else:
-            dma(qn, T.ti[16 * h:16 * h + 8, :], T.lam[:], [], ["ti"], "lt")
-        dma(qn, T.ti[16 * h + 9:16 * h + 16, :], T.rho[16:128, :], [], ["ti"], "lt")
-    dma("s", u8(T.wq[:, :]), T.wc[:], [], ["wq"], "lw")
-    dma("s", T.wp[:], T.ws[:], [], ["wq"], "lw")
-    dma("s", T.vv[:], T.v[:], [], ["vv"], "lv")
-
     def iota(out, pat, base, cm, W, f=True):
         kw = {"allow_small_or_imprecise_dtypes": True} if f else {}
         op("g", g.iota, (out, pat, base, cm), [], W, kw)
-    iota(T.ci[:, 0:1], [[0, 1]], 0, 1, ["ci0"], False)
-    iota(T.idt[:, :], [[1, 8], [0, 2], [8, 44]], 0, 0, ["idt"], False)
-    dma("y", T.ti[8:128:16, :], T.idt[0:8, :], ["idt"], ["ti"], "lt")
-    iota(T.fw[:, 0:4], [[16, 4]], 0, 0, ["fw"])
-    iota(T.fw[:, 4:8], [[1, 4]], 0, 0, ["fw"])
-    iota(T.fw[:, 8:12], [[32, 2], [48, 2]], 0, 0, ["fw"])
-    iota(T.fw[:, 12:16], [[2, 2], [4, 2]], 0, 0, ["fw"])
-    iota(T.fc[:, 0:64], [[32, 2], [48, 2], [1, 16]], 0, 0, ["fc"])
-    iota(T.fc[:, 64:128], [[2, 2], [4, 2], [32, 16]], 0, 0, ["fc"])
-    op("v", V.memset, (T.z8[:], 0.0), [], ["z8"])
 
-    def I(k):
-        return T.ci[:, k:k + 1]
+    spare = []
 
-    def F(k):
-        return T.cf[:, k:k + 1]
+    def gap(room=GAP):
+        while spare and spare[0][0] <= room + 1e-9:
+            cost, fn = spare.pop(0)
+            room -= cost
+            fn()
+
+    iota(T.ci[:, 0:8], [[6, 2], [0, 4]], 1, 1, ["cu"], False)
+    iota(T.idt[:, :], [[16, 44]], 0, 1, ["idt"], False)
+    iota(T.ci[:, 8:16], [[0, 8]], 0, 1, ["p"], False)
+    dma("s", T.ut[:], T.u[:], [], ["ut"], "lu")
+    for c, (c0, c1) in enumerate(XC):
+        dma("ys"[c], T.xt[:, 4 * c0:4 * c1], T.x[:, 4 * c0:4 * c1], [], ["xt%d" % c], "lx%d" % c)
+    for h in range(8):
+        nl, r0 = (8, 1) if h < 4 else (7, 0)
+        dma("y", T.ti[16 * h:16 * h + nl, :], T.lam[0:16 * nl, :], [], ["ti"], "lt")
+        dma("s", T.ti[16 * h + 8 + r0:16 * h + 16, :], T.rho[16 * r0:128, :], [], ["ti"], "lt")
+    dma("y", T.ti[8:64:16, :], T.idt[0:64, :], ["idt"], ["ti"], "lt")
+    dma("s", T.ti[71:128:16, :], T.idt[64:128, :], ["idt"], ["ti"], "lt")
+    dma("y", u8(T.wq[:, :]), T.wc[:], [], ["wq"], "lw")
+    dma("y", T.wp[:], T.ws[:], [], ["wq"], "lw")
+    dma("y", T.vv[:], T.v[:], [], ["vv"], "lv")
+
+    W_ = {"odd": (0, 6, [[16, 6]]), "even": (6, 6, [[32, 3], [96, 2]]), "t": (12, 16, [[1, 8], [0, 2]]), "e": (28, 2, [[8, 2]])}
+
+    def W(n):
+        return T.fw[:, W_[n][0]:W_[n][0] + W_[n][1]]
+    for n in ("odd", "even"):
+        iota(W(n), W_[n][2], 0, 0, ["w" + n])
+    iota(T.c3[:, :], [[3, 96]], 1, 0, ["c30"])
+    for n in ("t", "e"):
+        iota(W(n), W_[n][2], 0, 0, ["w" + n])
+    iota(T.tw[:, 0:1056:3], [[0, C]], 0, 0, ["twz"])
+    op("v", V.memset, (T.one[:], 1.0), [], ["one"])
+    col = {}
+
+    def F(n):
+        return T.cf[:, col[n]:col[n] + 1]
+
+    def const(n, a, s1, s2=None, o0=A.add, o1=None):
+        col[n] = len(col)
+        ts(F(n), F(a), F(s1) if s1 in col else s1, F(s2) if s2 in col else s2, o0, o1, [k for k in (a, s1, s2) if k in col], [n])
     SR, AND = A.logical_shift_right, A.bitwise_and
-    ts(I(1), I(0), 15, None, AND, None, ["ci0"], ["ci1"])
-    ts(I(2), I(0), 3, 1, SR, AND, ["ci0"], ["ci2"])
-    ts(I(3), I(0), 7, None, AND, None, ["ci0"], ["ci3"])
-    ts(I(4), I(0), 4, None, SR, None, ["ci0"], ["ci4"])
-    ts(I(5), I(0), 5, None, SR, None, ["ci0"], ["ci5"])
-    ts(I(6), I(0), 4, 1, SR, AND, ["ci0"], ["ci6"])
-    ts(I(7), I(2), -2, 1, A.mult, A.add, ["ci2"], ["ci7"])
-    tt(I(8), I(7), I(1), A.add, ["ci7", "ci1"], ["ci8"])
-    ts(I(9), I(8), 7, None, AND, None, ["ci8"], ["ci9"])
-    ts(F(0), I(9), 16.0, None, A.mult, None, ["ci9"], ["f0"])
-    ts(F(1), I(3), 16.0, 1.0, A.mult, A.add, ["ci3"], ["f1"])
-    ts(F(2), I(1), 7.0, -112.0, A.is_equal, A.mult, ["ci1"], ["f2"])
-    ts(T.ul[:, 0:8], T.z8[:], F(0), None, A.add, None, ["z8", "f0"], ["ul"])
-    ts(T.ul[:, 8:16], T.z8[:], F(1), None, A.add, None, ["z8", "f1"], ["ul"])
-    need("v", [("sv", total["sv"])])
-    ts(T.ul[:, 9:10], F(2), F(1), None, A.add, None, ["f1", "f2"], ["ul"])
-    ts(F(3), I(7), 1.0, None, A.mult, None, ["ci7"], ["f3"])
-    ts(F(4), I(0), 23.0, -2.0, A.is_equal, A.mult, ["ci0"], ["f4"])
-    tt(F(5), F(3), F(4), A.add, ["f3", "f4"], ["f5"])
-    tc(F(6), I(1), ["ci1"], ["f6"])
-    ts(F(7), I(1), 32.0, None, A.mult, None, ["ci1"], ["f7"])
-    tc(F(8), I(6), ["ci6"], ["f8"])
-    ts(F(9), I(4), 48.0, F(6), A.mult, A.add, ["ci4", "f6"], ["f9"])
-    ts(F(10), I(4), 4.0, F(7), A.mult, A.add, ["ci4", "f7"], ["f10"])
-    ts(F(11), I(6), 16.0, None, A.mult, None, ["ci6"], ["f11"])
-    ts(F(12), I(5), 96.0, F(11), A.mult, A.add, ["ci5", "f11"], ["f12"])
-    ts(F(13), I(5), 8.0, F(8), A.mult, A.add, ["ci5", "f8"], ["f13"])
-    tt(F(14), F(12), F(6), A.add, ["f12", "f6"], ["f14"])
-    tt(F(15), F(13), F(7), A.add, ["f13", "f7"], ["f15"])
-    for k, f in ((0, 9), (4, 10), (8, 14), (12, 15)):
-        ts(T.sl[:, k:k + 4], T.fw[:, k:k + 4], F(f), 351.0, A.add, A.min, ["fw", "f%d" % f], ["sl"])
-    ts(T.fc[:, 0:64], T.fc[:, 0:64], F(12), 351.0, A.add, A.min, ["fc", "f12"], ["fca"])
-    ts(T.fc[:, 64:128], T.fc[:, 64:128], F(13), 351.0, A.add, A.min, ["fc", "f13"], ["fca"])
-    ts(T.c3[:], T.fc[:], 3.0, None, A.mult, None, ["fca"], ["c3"])
-    ts(F(4), I(6), 352.0, None, A.mult, None, ["ci6", "f4", "f5"], ["hof"])
-    for k, val in ((0, 0), (1, 1), (2, -1)):
-        iota(T.d0[:, k:1056:3], [[0, C]], val, 0, ["phi" if k == 1 else "d0c"])
+    ts(T.ci[:, 16:24], T.ci[:, 0:8], 7, None, AND, None, ["cu"], ["cu7"])
+    parts = (("q", 0, 15), ("R", 6, 1), ("h", 4, 7), ("h3", 4, 3), ("a1", 5, 1), ("p32", 0, 31), ("q2", 1, 7), ("G", 4, 1), ("odd", 0, 1))
+    for k, (n, sh, m) in enumerate(parts):
+        col[n] = k
+        ts(T.ci[:, 32 + k:33 + k], T.ci[:, 8:9], sh, m, SR, AND, ["p"], ["ci"])
+        if k == 3:
+            ts(T.ul[:, 0:8], T.ci[:, 16:24], 16.0, None, A.mult, None, ["cu7"], ["ul0"])
+    tc(T.cf[:, 0:9], T.ci[:, 32:41], ["ci"], [n for n, sh, m in parts])
     quant(T.uq[:], T.us[:], T.ut[:], ["ut"], ["uq"])
-    op("v", V.tensor_copy, (T.pq[:, 0:256].bitcast(dt.uint32), T.uq[:, 0:128].bitcast(dt.uint32).indirect(T.ul[:, 0:16])), ["uq", "ul"], ["pq"])
-    act(T.ps[:, 0:256], T.us[:, 0:128].indirect(T.ul[:, 0:16]), ["uq", "ul"], ["pq"])
-    quant(T.xq[:], T.xs[:], T.xt[:], ["xt"], ["xq"])
+    const("y", "q", "R", 8.0, A.add, A.is_equal)
+    const("po", "h3", 96.0, "q", A.mult, A.add)
+    const("pe", "a1", 192.0, "p32", A.mult, A.add)
+    const("p3", "h3", 288.0, None, A.mult)
 
-    def scores(rows):
-        for k in rows:
-            mm(k, C, T.pq[:, 128 * k:128 * k + 128], T.ps[:, 128 * k:128 * k + 128], T.xq[:], T.xs[:], ["pq", "xq"])
-    scores([0])
-    for r in range(8):
-        e, o = T.ti[:, 88 * r:88 * r + 44], T.ti[:, 88 * r + 44:88 * r + 88]
-        tt(T.d1[:, 3 * r + 1:1056:24], o, e, A.add, ["ti"], ["d1s"])
-    for r in range(8):
-        e, o = T.ti[:, 88 * r:88 * r + 44], T.ti[:, 88 * r + 44:88 * r + 88]
-        tt(T.d1[:, 3 * r:1056:24], o, e, A.subtract, ["ti"], ["d1d"])
-    act(T.d1[:, 2:1056:3], T.d1[:, 1:1056:3], ["d1s"], ["d1n"], scale=3.0)
-    act(T.d1[:, 1:1056:3], T.d1[:, 1:1056:3], ["d1s"], ["d1m"], scale=1.5)
-    act(T.d1[:, 0:1056:3], T.d1[:, 0:1056:3], ["d1d"], ["d1b"], scale=1.5)
-    iota(T.rl[:, :], [[0, 2], [96, 16]], -287, 3, ["rli"])
-    iota(T.lw[:, :], [[3, 768]], 1, 0, ["lwz"])
-    iota(T.one[:, :], [[0, 512]], 1, 0, ["one"])
-    for b in range(4):
-        op("g", g.affine_select, (T.et[:, 512 * b:512 * b + 512], T.one[:], [[-1, 512]], A.is_equal, 0.0, b, 4), ["one"], ["et"])
+    def order_u(k):
+        op("v", V.tensor_copy, (T.pq[:, 128 * k:128 * k + 128].bitcast(dt.uint32), T.uq[:, 0:128].bitcast(dt.uint32).indirect(T.ul[:, 8 * k:8 * k + 8])), ["uq", "ul%d" % k], ["pq%d" % k])
+        act(T.ps[:, 128 * k:128 * k + 128], T.us[:, 0:128].indirect(T.ul[:, 8 * k:8 * k + 8]), ["uq", "ul%d" % k], ["pq%d" % k])
+    order_u(0)
+    for b in range(2):
+        act(T.et[:, 512 * b:512 * b + 512], T.one[:], ["one"], ["etz"], scale=0.0)
 
+    def pack_x(c):
+        c0, c1 = XC[c]
+        quant(T.xq[:, c0:c1], T.xs[:, c0:c1], T.xt[:, 4 * c0:4 * c1], ["xt%d" % c], ["xq%d" % c])
+
+    def scores(c, kinds):
+        c0, c1 = XC[c]
+        for k in kinds:
+            mm(2 * k + c, c1 - c0, T.pq[:, 128 * k:128 * k + 128], T.ps[:, 128 * k:128 * k + 128], T.xq[:, c0:c1], T.xs[:, c0:c1], ["pq%d" % k, "xq%d" % c])
+
+    def bits(c):
+        c0, c1 = XC[c]
+        ts(T.sb[:, c0:c1], bank(c, c1 - c0), 0.0, None, A.is_le, None, ["b%d" % c], ["sb"])
+
+    def first(c):
+        c0, c1 = XC[c]
+        ts(T.d0[:, 3 * c0 + 2:3 * c1:3], bank(4 + c, c1 - c0), F("thr"), F("half"), A.is_gt, A.subtract, ["b%d" % (4 + c), "thr", "half"], ["beta%d" % c])
+
+    def colours(c):
+        c0, c1 = XC[c]
+        act(T.d0[:, 3 * c0 + 1:3 * c1:3], bank(2 + c, c1 - c0), ["b%d" % (2 + c), "sgn"], ["phi%d" % c], SIGN, bias=2.0 ** -94, scale=F("sgn"))
+
+    def recolour(c):
+        c0, c1 = XC[c]
+        op("v", V.tensor_tensor_scan, (T.tw[:, 3 * c0:3 * c1], T.d0[:, 3 * c0:3 * c1], T.d1[:, 3 * c0:3 * c1], 0.0, A.mult, A.add),
+           ["d0c", "phi%d" % c, "beta%d" % c, "d1b", "d1m", "d1n"], ["tw%d" % c])
+    for c in range(2):
+        pack_x(c)
+        scores(c, [0])
+    const("e", "y", -1.5, None, A.mult)
+    const("q5", "q", 5.0, 16.0, A.min, A.mult)
+    ts(T.mp[:, 0:6], W("odd"), F("po"), 351.0, A.add, A.min, ["wodd", "po"], ["mpo"])
+    ts(T.gr[:, 0:6], W("even"), F("pe"), 351.0, A.add, A.min, ["weven", "pe"], ["me"])
+    ts(T.c3[:], T.c3[:], F("p3"), 1054.0, A.add, A.min, ["c30", "p3"], ["c3"])
+    const("sg", "R", -2.0, 1.0, A.mult, A.add)
+    const("h24", "h", "e", 16.0, A.mult, A.mult)
+    const("sb0", "R", 15.0, "q5", A.mult, A.add)
+    const("scale", "e", 3.0, None, A.add)
+    tc(T.mp[:, 6:12], T.gr[:, 0:6], ["me"], ["mpe"])
+    for c in range(2):
+        bits(c)
+    const("even0", "h24", 1.0, None, A.add)
+    const("odd0", "h24", "e", 1.0, A.add, A.add)
+    ts(T.sel[:], W("t"), F("sg"), F("sb0"), A.mult, A.add, ["wt", "sg", "sb0"], ["sel"])
+    const("q6", "q2", 5.0, 16.0, A.min, A.mult)
+
+    def windows(rs):
+        for r in rs:
+            ts(T.tw[:, 3 * r + 2:1056:24], T.ti[:, 88 * r:88 * r + 44], F("scale"), F("even0"), A.mult, A.add, ["ti", "scale", "even0"], ["tw0", "tw1"])
+            ts(T.tw[:, 3 * r + 1:1056:24], T.ti[:, 88 * r + 44:88 * r + 88], F("scale"), F("odd0"), A.mult, A.add, ["ti", "scale", "odd0"], ["tw0", "tw1"])
+
+    def places(t, n=96):
+        tc(T.off[:], T.zm[:, 0:n].indirect(T.sel[:, 2 * t:2 * t + 1]), ["zm", "sel"], ["off"])
+    tt(T.gm[:, 0:96], T.sb[:].indirect(T.mp[:, 0:6]), T.c3[:], A.add, ["sb", "mpo", "c3"], ["gm"])
+    windows((0, 1))
+    turn(T.zm[:, 0:96], T.gm[:, 0:96], ["gm"], ["zm"])
+    windows((2, 3))
+    places(7)
+    windows((4, 5, 6, 7))
+    iota(T.lw[:, :], [[0, 768]], 1, 0, ["lwz"])
+    iota(T.zb[:, 352:384], [[0, 32]], 0, 0, ["zbz"])
+    op("g", g.affine_select, (T.eye[:], T.one[:, 0:128], [[-1, 128]], A.is_equal, 0.0, 0, 1), ["one"], ["eye"])
     iota(T.yw[:, :], [[1, 22], [22, 16]], 0, 0, ["yw0"])
-    iota(T.lk[:, :], [[0, 704]], 0, 0, ["lkz"], False)
-    K12 = (T.ko[:, 0:CH[0][1] // 16], T.ko[:, CH[0][1] // 16:22])
+    iota(T.lk[:, :], [[0, 704]], 0, 0, ["lkz"])
+    iota(T.d0[:, 0:1056:3], [[0, C]], 0, 0, ["d0c"])
+
+    def later(cost, fn, *a):
+        spare.append((cost, lambda: fn(*a)))
+    SMALL = 0.06
+    later(SMALL, const, "s5", "R", 5.0, 5.0, A.mult, A.add)
+    later(SMALL, lambda: op("v", V.memset, (T.ro[:], 0), [], ["roz"]))
+    later(SMALL, const, "x", "R", -15.0, "q", A.mult, A.add)
+    later(SMALL, lambda: ts(T.sel[:, 10:11], F("s5"), F("q6"), None, A.add, None, ["s5", "q6", "sel"], ["sel5"]))
+    later(SMALL, lambda: ts(T.gr[:, 8:10], W("e"), F("q2"), 10.0, A.add, A.min, ["we", "q2"], ["fb"]))
+    later(SMALL, const, "ne", "x", 0.0, None, A.not_equal)
+    later(SMALL, const, "hm", "h", -3.5, None, A.add)
+    later(SMALL, lambda: ts(T.gr[:, 10:12], T.gr[:, 8:10], 6.0, -6.0, A.is_ge, A.mult, ["fb"], ["f6"]))
+    later(SMALL, const, "o16", "odd", 16.0, None, A.mult)
+    later(SMALL, const, "hh", "hm", "hm", 12.0, A.mult, A.is_gt)
+    later(SMALL, lambda: tt(T.gr[:, 12:14], T.gr[:, 8:10], T.gr[:, 10:12], A.add, ["fb", "f6"], ["f7"]))
+    later(SMALL, const, "thr", "ne", 1e29, None, A.mult)
+    later(SMALL, const, "half", "ne", 1.0, 0.5, A.add, A.mult)
+    later(SMALL, lambda: ts(T.gr[:, 14:16], T.gr[:, 12:14], 3.0, -5.0, A.is_ge, A.mult, ["f7"], ["f8"]))
+    later(SMALL, lambda: tt(T.gr[:, 16:18], T.gr[:, 12:14], T.gr[:, 8:10], A.add, ["f7", "fb"], ["f9"]))
+    later(SMALL, const, "ff", "hh", -0.9375, 1.0, A.mult, A.add)
+    later(SMALL, const, "fo", "hh", 352.0, None, A.mult)
+    later(SMALL, lambda: tt(T.gr[:, 18:20], T.gr[:, 16:18], T.gr[:, 14:16], A.add, ["f9", "f8"], ["f10"]))
+    later(SMALL, const, "hof", "G", 352.0, None, A.mult)
+    later(SMALL, const, "msc", "ne", 0.5, None, A.mult)
+    later(SMALL, lambda: ts(T.gr[:, 20:22], T.gr[:, 18:20], 32.0, F("o16"), A.mult, A.add, ["f10", "o16"], ["f11"]))
+    later(SMALL, const, "bsc", "half", -1.0, 1.5, A.mult, A.add)
+    later(SMALL, const, "sgn", "q", 8.0, 0.5, A.is_lt, A.subtract)
+    later(SMALL, lambda: ts(T.fin[:], T.gr[:, 20:22], F("ff"), F("fo"), A.mult, A.add, ["f11", "ff", "fo"], ["fin"]))
+    later(SMALL, lambda: ts(T.ci[:, 24:32], T.ci[:, 8:16], 7, None, AND, None, ["p"], ["cc7"]))
+    later(SMALL, lambda: op("v", V.memset, (T.ul[:, 16:20], 0), [], ["ul2"]))
+    later(SMALL, lambda: op("v", V.memset, (T.ul[:, 20:24], 112), [], ["ul2"]))
+    later(SMALL, lambda: ts(T.ul[:, 8:16], T.ci[:, 24:32], 16.0, 1.0, A.mult, A.add, ["cc7"], ["ul1"]))
+    later(SMALL, lambda: ts(T.mp[:, 12:18], T.gr[:, 0:6], 3.0, 2.0, A.mult, A.add, ["me"], ["mp0"]))
 
     def plane(t, b, c0=0, c1=C):
         return t[:, C * b + c0:C * b + c1]
@@ -234,62 +309,65 @@ def rank_program(g, core, T, topo):
     def inter(t, b, c0=0, c1=C):
         return t[:, 4 * c0 + b:4 * c1:4]
 
+    def halves(k, o):
+        lo, hi = 264 * k, 264 * k + 264
+        if o == "sum":
+            tt(T.sm[:, 88 * k:88 * k + 88], T.tw[:, lo + 1:hi:3], T.tw[:, lo + 2:hi:3], A.add, ["tw0", "tw1"], ["sm"])
+        elif o == "diff":
+            tt(T.d1[:, lo:hi:3], T.tw[:, lo + 1:hi:3], T.tw[:, lo + 2:hi:3], A.subtract, ["tw0", "tw1"], ["d1d"])
+        else:
+            tt(T.d1[:, lo:hi:3], T.tw[:, lo + 1:hi:3], T.d1[:, lo + 1:hi:3], A.subtract, ["tw0", "tw1", "d1m"], ["d1b"])
+
     for rnd in range(3):
         partner = T.cores[rank ^ STEP[rnd]]
-        if rnd:
-            op("s", S.activation, (T.d0[:, 1:1056:3], bank(1), SIGN), ["b1", "f5"], ["phi"], {"bias": 2.0 ** -94, "scale": F(5)})
-        ts(T.sb[:], bank(0), 0.0, 1.0, A.is_le, A.add, ["b0"], ["sb"])
-        tt(T.gm[:], T.sb[:].indirect(T.sl[:, 8:16]), T.c3[:], A.add, ["sb", "sl", "c3"], ["gm"])
-
-        def wrap(src, key, ql, qr):
-            z = "zm" if key == "gm" else "zt"
-            op("v", V.transpose, (T[z][:], src), [key], [z])
-            tc(T.off[:, 0:4], T[z][:, ql:64:16], [z], ["off"])
-            tc(T.off[:, 4:8], T[z][:, 64 + qr:128:16], [z], ["off"])
-        wrap(T.gm[:], "gm", 7, 8)
-        act(T.bra[:], T.sb[:].indirect(T.sl[:, 0:8]), ["sb", "sl"], ["bra"])
-        act(T.brb[:], T.sb[:].indirect(T.sl[:, 8:16]), ["sb", "sl"], ["brb"])
-        for b in range(4):
-            act(plane(T.xh, b), inter(T.xt, b), ["xt"], ["xh%d" % b], scale=0.5)
-        act(T.xi[:], T.xt[:], ["xt"], ["xi"], scale=0.5)
-        op("v", V.tensor_tensor_scan, (T.tw[:], T.d0[:], T.d1[:], 0.0, A.mult, A.add), ["d0c", "phi", "d1b", "d1m", "d1n"], ["tw"])
         hop = "hop%d" % rnd
-
-        def land(qn, gt, key, lists):
-            for kind, q, to in lists:
-                a, h = to // 2, to % 2
-                if kind == "l":
-                    for d in (0, 16):
-                        dma(qn[0], T.lw[32 * a + d:32 * a + d + 1, 384 * h:384 * h + 384], gt[q:128:16, 0:48], [key, "lwz"], ["lw"], hop)
-                        qn = qn[1:] + qn[:1]
-                else:
-                    dma(qn[0], T.rl[32 * a:32 * a + 32, 16 * h:16 * h + 16], gt[q:128:16, 64:128], [key, "rli"], ["rl"], hop)
-                    qn = qn[1:] + qn[:1]
-        for t in range(7):
-            name = "gm" if t % 2 else "g%d" % t
-            tt(T[name][:], T.tw[:].indirect(T.off[:, 0:8]), (T.brb if t % 2 else T.bra)[:], A.add, ["tw", "off", "brb" if t % 2 else "bra"], [name])
-            if t < 6:
-                wrap(T[name][:], name, t, 15 - t)
-            if t % 2 == 0:
-                todo = [("l", t, t + 1), ("r", 15 - t, 6 - t)]
-                if t:
-                    todo += [("l", 8, t), ("r", 8, 7 - t)]
-                land("y" if t < 6 else "ys", T[name], name, todo)
+        act(T.bra[:], T.sb[:].indirect(T.mp[:, 6:12]), ["sb", "mpe"], ["bra"])
+        act(T.brb[:], T.sb[:].indirect(T.mp[:, 0:6]), ["sb", "mpo"], ["brb"])
+        for b in range(4):
+            act(plane(T.xh, b), inter(T.xt, b), ["xt0", "xt1"], ["xh%d" % b], scale=0.5)
+        act(T.xi[:], T.xt[:], ["xt0", "xt1"], ["xi"], scale=0.5)
         if rnd:
-            tt(T.d1[:, 0:1056:3], T.d1[:, 0:1056:3], T.d0[:, 1:1056:3], A.mult, ["d1b", "phi"], ["d1b"])
-        else:
-            quant(T.eq[:], T.es[:], T.et[:], ["et"], ["eq"])
+            for k in range(4):
+                later(0.16, halves, k, "b")
         if rnd == 2:
-            quant(T.zq[:], T.zs[:], T.vv[:], ["vv"], ["zq"])
-        if rnd == 0:
-            ts(T.yw[:], T.yw[:], F(4), None, A.add, None, ["yw0", "hof"], ["yw"])
-        for h in range(2):
-            ts(T.ro[:, h:22:2], T.rl[:, 16 * h:16 * h + 11], 1152.0 * h - 1.0, 1.0 / 3.0, A.add, A.mult, ["rl", "rli"], ["ro"])
-        tc(T.gcm[:], T.lw[:].indirect(T.ro[:]), ["lw", "lwz", "ro"], ["gcm"])
-        op("v", V.transpose, (T.zc[:], T.gcm[:]), ["gcm"], ["zc"])
+            later(0.14, quant, T.zq[:], T.zs[:], T.vv[:], ["vv"], ["zq"])
+        for t in range(6):
+            name = "g%d" % t if t % 2 else "gm"
+            gt, br = T[name][:, 0:96], "brb" if t % 2 else "bra"
+            lst, key = (T.mp[:, 12:18], "mp0") if t == 0 and rnd else (T.off[:, 0:6], "off")
+            tt(gt, T.tw[:].indirect(lst), T[br][:], A.add, ["tw0", "tw1", "twz", key, br], [name])
+            if t % 2:
+                for n, (q, to, d) in enumerate(((t, t + 1, 0), (t, t + 1, 16), (8, t, 0), (8, t, 16))):
+                    p = 32 * (to // 2) + d
+                    dma("ys"[n % 2] if t == 5 else "y", T.lw[p:p + 1, 384 * (to % 2):384 * (to % 2) + 384], T[name][q:64:16, :], [name, "lwz"], ["lw"], hop)
+            gap()
+            turn(T.zm[:, 0:96], gt, [name], ["zm"])
+            gap()
+            if t == 5:
+                need("v", gens["sel5"][1])
+            places(t)
+            if t % 2:
+                for j, to in ((15 - t, 6 - t), (7, 7 - t)):
+                    p, s = 32 * (to // 2), to % 2
+                    for a in range(2):
+                        n = 6 - a
+                        ts(T.ro[p:p + 32, 12 * a + s:12 * a + 2 * n:2], T.zm[64 + 32 * a:96 + 32 * a, j:16 * n:16], 1152.0 * s - 1.5, 1.0 / 3.0, A.add, A.mult, ["zm", "roz"], ["ro"])
+            else:
+                gap()
+        act(T.gb[:], T.lw[:].indirect(T.ro[:]), ["lw", "lwz", "ro", "roz"], ["gb"], IDENT, scale=1.0 / 3.0, bias=-MID - 0.5)
+        tc(T.gm[:], T.tw[:].indirect(T.off[:, 0:12]), ["tw0", "tw1", "twz", "off"], ["gm"])
+        gap()
+        turn(T.zm[:], T.gm[:], ["gm"], ["zm"])
+        gap()
+        for p, j, p0 in ((96, 6, 0), (0, 9, 64)):
+            for a in range(2):
+                ts(T.zb[p:p + 32, 352 + 12 * a:364 + 12 * a], T.zm[p0 + 32 * a:p0 + 32 * a + 32, j:192:16], -3.0 * MID - 1.0, 1.0 / 3.0, A.add, A.mult, ["zm", "zbz"], ["zbx"])
+        turn(T.zb[:, 0:352], T.gb[:], ["gb"], ["zb"])
+        gap()
         ki, kk = T["ki%d" % rnd], "ki%d" % rnd
-        ts(ki[:], T.zc[:, 0:352:16], -1.0, 1.0 / 3.0, A.add, A.mult, ["zc"], [kk])
-        ts(T.ko[:], T.zc[:, 0:352:16], -1.0, 1.0 / 3.0, A.add, A.mult, ["zc"], ["ko"])
+        ts(T.ko[:], T.zb[:].indirect(T.fin[:]), float(MID), None, A.add, None, ["zb", "zbx", "zbz", "fin"], ["ko"])
+        act(ki[:], T.zb[:].indirect(T.fin[:]), ["zb", "zbx", "zbz", "fin"], [kk])
+        gap()
         rid, pid = topo.addr(partner)[0:2]
         mask = topo.mask(core, partner)
         ne = len(topo.engines(core, partner))
@@ -306,31 +384,59 @@ def rank_program(g, core, T, topo):
             quant(hq[:, c0:c1], hs[:, c0:c1], T.hl[:, 4 * c0:4 * c1], ["hl%d" % c], ["hq%d%d" % (rnd, c)])
             send(u8(aq[:, c0:c1]), u8(hq[:, c0:c1]), "arr%d%d" % (rnd, c), "hq%d%d" % (rnd, c))
             send(as_[:, c0:c1], hs[:, c0:c1], "arr%d%d" % (rnd, c), "hq%d%d" % (rnd, c))
-        send(T["ka%d" % rnd][:], ki[:], "ark%d" % rnd, kk)
-        for c, (c0, c1) in enumerate(CH):
-            for b in range(4):
-                if c == 1 and b == LATE:
-                    send_h(0)
-                tt(inter(T.vt, b, c0, c1), plane(T.xh, b).indirect(K12[c]), inter(T.xi, b, c0, c1), A.add, ["xh%d" % b, "xi", "ko"], ["vt%d" % c])
+        send(T["ka%d" % rnd][:], ki[:, 0:22], "ark%d" % rnd, kk)
+        if rnd == 0:
+            act(T.yw[:], T.yw[:], ["yw0", "hof"], ["yw"], IDENT, bias=F("hof"))
+        act(T.gh[:], T.yw[:].indirect(T.ko[:, 0:22]), ["yw", "ko"], ["gh"])
+
+        def make_v(c, b):
+            c0, c1 = CH[c]
+            tt(inter(T.vt, b, c0, c1), plane(T.xh, b).indirect(T.ko[:, c0 // 16:c1 // 16]), inter(T.xi, b, c0, c1), A.add, ["xh%d" % b, "xi", "ko"], ["vt%d" % c])
+
+        def layer(c):
+            c0, c1 = CH[c]
             quant(T.vq[:, c0:c1], T.vs[:, c0:c1], T.vt[:, 4 * c0:4 * c1], ["vt%d" % c], ["vq%d" % c])
             for b in range(4):
                 mm(4 * c + b, c1 - c0, T.wq[:, 128 * b:128 * b + 128], T.wp[:, 128 * b:128 * b + 128], T.vq[:, c0:c1], T.vs[:, c0:c1], ["wq", "vq%d" % c])
                 if c == 0 or b % 2:
                     act(inter(T.hl, b, c0, c1), bank(4 * c + b, c1 - c0), ["b%d" % (4 * c + b)], ["hl%d" % c], scale=0.03125)
-            if c == PLACES:
-                tc(T.gcm[:], T.yw[:].indirect(T.ko[:]), ["yw", "ko"], ["gcm"])
-            if c == 1:
-                for b in (0, 2):
-                    ts(inter(T.hl, b, c0, c1), bank(4 + b, c1 - c0), 0.03125, None, A.mult, None, ["b%d" % (4 + b)], ["hl1"])
-                send_h(1)
+        for b in range(4):
+            make_v(0, b)
+        make_v(1, 0)
+        layer(0)
+        for b in range(1, 4):
+            make_v(1, b)
+        turn(T.zh[:], T.gh[:], ["gh"], ["zh"])
+        layer(1)
+        tc(T.roe[:], T.zh[:, 0:352:16], ["zh"], ["roe"])
+        send_h(0)
+        for b in (0, 2):
+            ts(inter(T.hl, b, CH[1][0], CH[1][1]), bank(4 + b, CH[1][1] - CH[1][0]), 0.03125, None, A.mult, None, ["b%d" % (4 + b)], ["hl1"])
+        send_h(1)
         for d in (0, 16):
             need("y", [("ark%d" % rnd, None)])
             dma("y", T.lk[d:128:32, :], T["ka%d" % rnd][:], ["lkz"], ["lk"], "kop%d" % rnd)
-        op("v", V.transpose, (T.zc[:], T.gcm[:]), ["gcm"], ["zc"])
-        tc(T.roe[:], T.zc[:, 0:352:16], ["zc"], ["roe"])
-        tc(T.gcm[:], T.lk[:].indirect(T.roe[:]), ["lk", "lkz", "roe"], ["gcm"])
-        op("v", V.transpose, (T.zc[:], T.gcm[:]), ["gcm"], ["zc"])
-        tc(T.eo[:], T.zc[:, 0:352:16], ["zc"], ["eo"])
+        tc(T.ge[:], T.lk[:].indirect(T.roe[:]), ["lk", "lkz", "roe"], ["ge"])
+        if rnd == 0:
+            for b in (2, 3):
+                act(T.et[:, 512 * b:512 * b + 512], T.one[:], ["one"], ["etz"], scale=0.0)
+            for b in range(4):
+                act(T.et[:, 512 * b + b:512 * b + 512:4], T.eye[:], ["eye", "etz"], ["et"])
+            for o in ("sum", "diff"):
+                for k in range(4):
+                    later(0.16, halves, k, o)
+            later(0.2, order_u, 1)
+            later(0.2, order_u, 2)
+        gap()
+        turn(T.ze[:], T.ge[:], ["ge"], ["ze"])
+        gap()
+        ts(T.eo[:], T.ze[:, 0:352:16], float(MID), None, A.add, None, ["ze"], ["eo"])
+        gap(9.0)
+        if rnd == 0:
+            quant(T.eq[:], T.es[:], T.et[:], ["et", "etz"], ["eq"])
+            act(T.d1[:, 2:1056:3], T.sm[:], ["sm", "half"], ["d1n"], scale=F("half"))
+            act(T.d1[:, 1:1056:3], T.sm[:], ["sm", "msc"], ["d1m"], scale=F("msc"))
+            act(T.d1[:, 0:1056:3], T.d1[:, 0:1056:3], ["d1d", "bsc"], ["d1b"], scale=F("bsc"))
         for c, (c0, c1) in enumerate(CH):
             need("t", [("arr%d%d" % (rnd, c), None)])
             for b in range(4):
@@ -339,22 +445,43 @@ def rank_program(g, core, T, topo):
                     act(plane(T.dp, b, c0, c1), bank(4 * c + b, c1 - c0), ["b%d" % (4 * c + b)], ["dp%d" % b])
                 else:
                     tc(plane(T.dp, b, c0, c1), bank(4 * c + b, c1 - c0), ["b%d" % (4 * c + b)], ["dp%d" % b])
-        for b in (0, 2, 1, 3):
-            tt(inter(T.xt, b), plane(T.dp, b).indirect(T.eo[:]), inter(T.vt, b), A.add, ["dp%d" % b, "eo", "vt0", "vt1"], ["xt"])
-        quant(T.xq[:], T.xs[:], T.xt[:], ["xt"], ["xq"])
-        scores([0, 1] if rnd < 2 else [1])
 
-    mm(2, C, T.zq[:], T.zs[:], T.xq[:], T.xs[:], ["zq", "xq"])
-    dma("y", T.oc[:], u8(T.xq[:, :]), ["xq"], [], "outs")
+        def make_x(c, b):
+            c0, c1 = XC[c]
+            tt(inter(T.xt, b, c0, c1), plane(T.dp, b).indirect(T.eo[:, c0 // 16:c1 // 16]), inter(T.vt, b, c0, c1), A.add, ["dp%d" % b, "eo", "vt0", "vt1"], ["xt%d" % c])
+        more = rnd < 2
+        for b in (0, 2, 1, 3):
+            make_x(0, b)
+        make_x(1, 0)
+        pack_x(0)
+        scores(0, [1, 2, 0] if more else [1])
+        colours(0)
+        for b in (2, 1, 3):
+            make_x(1, b)
+        if more:
+            first(0)
+        pack_x(1)
+        scores(1, [1, 2, 0] if more else [1])
+        colours(1)
+        if more:
+            bits(0)
+        recolour(0)
+        if more:
+            first(1)
+            bits(1)
+            recolour(1)
+
+    mm(4, C, T.zq[:], T.zs[:], T.xq[:], T.xs[:], ["zq", "xq0", "xq1"])
+    dma("y", T.oc[:], u8(T.xq[:, :]), ["xq0", "xq1"], [], "outs")
     for k in range(4):
-        dma("y", T.osc[4 * k:4 * k + 4, :], T.xs[32 * k:32 * k + 4, :], ["xq"], [], "outs")
-    op("s", S.activation, (T.d0[:, 1:1056:3], bank(1), SIGN), ["b1", "f5"], ["phi"], {"bias": 2.0 ** -94, "scale": F(5)})
-    tc(T.yt[:], bank(2), ["b2"], ["yt"])
-    dma("y", T.y[:], T.yt[:], ["yt"], [], "outs")
-    op("v", V.tensor_tensor_scan, (T.tw[:], T.d0[:], T.d1[:], 0.0, A.mult, A.add), ["d0c", "phi", "d1b", "d1m", "d1n"], ["tw"])
-    ts(T.lt[:, 0:704:2], T.tw[:, 2:1056:3], 1.0 / 3.0, None, A.mult, None, ["tw"], ["lt"])
-    act(T.lt[:, 1:704:2], T.tw[:, 1:1056:3], ["tw"], ["lt"], scale=1.0 / 3.0)
-    dma("y", T.lr[0:8, 0:704], T.lt[0:8, :], ["lt"], [], "outs")
-    dma("s", T.lr[1:8, 704:1408], T.lt[9:16, :], ["lt"], [], "outs")
-    dma("s", T.lr[0:1, 704:1408], T.lt[23:24, :], ["lt"], [], "outs")
+        dma("y", T.osc[4 * k:4 * k + 4, :], T.xs[32 * k:32 * k + 4, :], ["xq0", "xq1"], [], "outs")
+    act(T.yt[:], bank(4, C), ["b4"], ["yt"])
+    dma("s", T.y[:], T.yt[:], ["yt"], [], "outs")
+    recolour(1)
+    ts(T.lt[:, 0:704:2], T.tw[:, 2:1056:3], -1.0, 1.0 / 3.0, A.add, A.mult, ["tw0", "tw1"], ["lt"])
+    ts(T.lt[:, 1:704:2], T.tw[:, 1:1056:3], -1.0, 1.0 / 3.0, A.add, A.mult, ["tw0", "tw1"], ["lt"])
+    dma("y", T.lr[1:8, 0:704], T.lt[1:8, :], ["lt"], [], "outs")
+    dma("s", T.lr[0:7, 704:1408], T.lt[72:79, :], ["lt"], [], "outs")
+    dma("y", T.lr[0:1, 0:704], T.lt[64:65, :], ["lt"], [], "outs")
+    dma("s", T.lr[7:8, 704:1408], T.lt[15:16, :], ["lt"], [], "outs")
     need("g", [(s, None) for s in total if not s.startswith("ar")])

from concourse.bass import DstId, RemoteDMATransfer
from concourse.mybir import dt, AluOpType, ActivationFunctionType

C = 352
STEP = (1, 2, 4)
CH = ((0, 224), (224, 352))
XC = ((0, 192), (192, 352))
LATE = 3
MID = 176
GAP = 0.2
A = AluOpType
COPY = ActivationFunctionType.Copy
IDENT = ActivationFunctionType.Identity
SIGN = ActivationFunctionType.Sign
F8 = "float8_e4m3fn_x4"

SCRATCH = {
    "xt": ("sbuf", [128, 4 * C], "bfloat16"), "xh": ("sbuf", [128, 4 * C], "bfloat16"), "xi": ("sbuf", [128, 4 * C], "bfloat16"),
    "vt": ("sbuf", [128, 4 * C], "bfloat16"), "hl": ("sbuf", [128, 4 * C], "bfloat16"), "dp": ("sbuf", [128, 4 * C], "bfloat16"),
    "ut": ("sbuf", [128, 512], "bfloat16"), "vv": ("sbuf", [128, 512], "bfloat16"), "et": ("sbuf", [128, 2048], "bfloat16"),
    "one": ("sbuf", [128, 512], "bfloat16"), "eye": ("sbuf", [128, 128], "bfloat16"),
    "xq": ("sbuf", [128, C], F8), "xs": ("sbuf", [128, C], "uint8"),
    "vq": ("sbuf", [128, C], F8), "vs": ("sbuf", [128, C], "uint8"),
    "uq": ("sbuf", [128, 128], F8), "us": ("sbuf", [128, 128], "uint8"),
    "pq": ("sbuf", [128, 384], F8), "ps": ("sbuf", [128, 384], "uint8"),
    "zq": ("sbuf", [128, 128], F8), "zs": ("sbuf", [128, 128], "uint8"),
    "eq": ("sbuf", [128, 512], F8), "es": ("sbuf", [128, 512], "uint8"),
    "wq": ("sbuf", [128, 512], F8), "wp": ("sbuf", [128, 512], "uint8"),
    "ti": ("sbuf", [128, 704], "int32"), "idt": ("sbuf", [128, 44], "int32"),
    "d0": ("sbuf", [128, 1056], "float32"), "d1": ("sbuf", [128, 1056], "float32"), "tw": ("sbuf", [128, 1056], "float32"),
    "sm": ("sbuf", [128, C], "float32"), "sb": ("sbuf", [128, C], "float32"),
    "bra": ("sbuf", [128, 96], "float32"), "brb": ("sbuf", [128, 96], "float32"), "c3": ("sbuf", [128, 96], "float32"),
    "gm": ("sbuf", [128, 192], "float32"), "g1": ("sbuf", [128, 96], "float32"), "g3": ("sbuf", [128, 96], "float32"), "g5": ("sbuf", [128, 96], "float32"),
    "zm": ("sbuf", [128, 192], "float32"),
    "off": ("sbuf", [128, 16], "uint16"), "mp": ("sbuf", [128, 18], "uint16"), "ul": ("sbuf", [128, 24], "uint16"),
    "sel": ("sbuf", [128, 16], "uint16"), "fin": ("sbuf", [128, 2], "uint16"),
    "lw": ("sbuf", [128, 768], "float32"), "ro": ("sbuf", [128, 22], "uint16"),
    "gb": ("sbuf", [128, C], "bfloat16"), "zb": ("sbuf", [128, 384], "bfloat16"), "gh": ("sbuf", [128, C], "float16"), "zh": ("sbuf", [128, C], "float16"),
    "ge": ("sbuf", [128, C], "bfloat16"), "ze": ("sbuf", [128, C], "bfloat16"),
    "ko": ("sbuf", [128, 32], "uint16"), "yw": ("sbuf", [128, C], "float32"), "roe": ("sbuf", [128, 22], "uint16"), "eo": ("sbuf", [128, 22], "uint16"),
    "lk": ("sbuf", [128, 704], "bfloat16"),
    "ci": ("sbuf", [128, 48], "int32"), "cf": ("sbuf", [128, 48], "float32"), "gr": ("sbuf", [128, 32], "float32"), "fw": ("sbuf", [128, 32], "float32"),
    "yt": ("sbuf", [128, C], "float32"), "lt": ("sbuf", [128, 704], "float32"),
    "pm": ("psum", [128, 4096], "float32"),
}
for _r in range(3):
    SCRATCH["hq%d" % _r] = ("sbuf", [128, C], F8)
    SCRATCH["hs%d" % _r] = ("sbuf", [128, C], "uint8")
    SCRATCH["aq%d" % _r] = ("sbuf", [128, C], F8)
    SCRATCH["as%d" % _r] = ("sbuf", [128, C], "uint8")
    SCRATCH["ki%d" % _r] = ("sbuf", [128, 32], "bfloat16")
    SCRATCH["ka%d" % _r] = ("sbuf", [128, 22], "bfloat16")
SEMAPHORES = (["sv", "ss", "st", "sg", "lu", "lx0", "lx1", "lt", "lw", "lv", "snt", "outs"]
              + [n % r for r in range(3) for n in ("hop%d", "kop%d", "ark%d")] + ["arr%d%d" % (r, c) for r in range(3) for c in range(2)])


def rank_program(g, core, T, topo):
    rank = T.rank_of(core)
    if rank is None:
        return
    Q = {"v": g.vector, "s": g.scalar, "t": g.tensor, "g": g, "y": g.sync}
    SEM = {"v": "sv", "s": "ss", "t": "st", "g": "sg"}
    total = {}
    waited = {}
    gens = {}

    def need(qn, toks):
        best = {}
        for s, n in toks:
            n = total[s] if n is None else n
            best[s] = max(best.get(s, 0), n)
        for s, n in best.items():
            if waited.get((qn, s), 0) < n:
                Q[qn].wait_ge(T.sem[s], n)
                waited[(qn, s)] = n

    def before(qn, R, W, own=None):
        toks = []
        for k in R:
            toks += gens.setdefault(k, [[], [], []])[1]
        for k in W:
            e = gens.setdefault(k, [[], [], []])
            if e[2]:
                gens[k] = e = [e[1] + e[2], [], []]
            toks += [t for t in e[0] if t[0] != own]
        need(qn, toks)

    def after(tok, R, W):
        for k in R:
            gens[k][2].append(tok)
        for k in W:
            gens[k][1].append(tok)

    def op(qn, fn, args, R, W, kw=None):
        s = SEM[qn]
        before(qn, R, W, s)
        fn(*args, **(kw or {})).then_inc(T.sem[s], 1)
        total[s] = total.get(s, 0) + 1
        after((s, total[s]), R, W)

    def dma(qn, out, in_, R, W, sem):
        before(qn, R, W)
        Q[qn].dma_start(out, in_).then_inc(T.sem[sem], 16)
        total[sem] = total.get(sem, 0) + 16
        after((sem, None), R, W)

    V, S, TE = g.vector, g.scalar, g.tensor

    def ts(out, in0, s1, s2, o0, o1, R, W):
        if o1 is None:
            op("v", V.tensor_scalar, (out, in0, s1, None, o0), R, W)
        else:
            op("v", V.tensor_scalar, (out, in0, s1, s2, o0, o1), R, W)

    def tt(out, a, b, o, R, W):
        op("v", V.tensor_tensor, (out, a, b, o), R, W)

    def tc(out, a, R, W):
        op("v", V.tensor_copy, (out, a), R, W)

    def turn(out, a, R, W):
        op("v", V.transpose, (out, a), R, W)

    def act(out, a, R, W, fn=COPY, **kw):
        op("s", S.activation, (out, a, fn), R, W, kw)

    def bank(i, n):
        return T.pm[:, 512 * i:512 * i + n]

    def mm(i, n, lq, ls, rq, rs, R):
        op("t", TE.matmul_mx, (bank(i, n), lq, ls, rq, rs, True, True), R, ["b%d" % i])

    def quant(q, s, t, R, W):
        op("v", V.quantize_mx, (q, s, t), R, W)

    def u8(v):
        return v.bitcast(dt.uint8)

    def iota(out, pat, base, cm, W, f=True):
        kw = {"allow_small_or_imprecise_dtypes": True} if f else {}
        op("g", g.iota, (out, pat, base, cm), [], W, kw)

    spare = []

    def gap(room=GAP):
        while spare and spare[0][0] <= room + 1e-9:
            cost, fn = spare.pop(0)
            room -= cost
            fn()

    iota(T.ci[:, 0:8], [[6, 2], [0, 4]], 1, 1, ["cu"], False)
    iota(T.idt[:, :], [[16, 44]], 0, 1, ["idt"], False)
    iota(T.ci[:, 8:16], [[0, 8]], 0, 1, ["p"], False)
    dma("s", T.ut[:], T.u[:], [], ["ut"], "lu")
    for c, (c0, c1) in enumerate(XC):
        dma("ys"[c], T.xt[:, 4 * c0:4 * c1], T.x[:, 4 * c0:4 * c1], [], ["xt%d" % c], "lx%d" % c)
    for h in range(8):
        nl, r0 = (8, 1) if h < 4 else (7, 0)
        dma("y", T.ti[16 * h:16 * h + nl, :], T.lam[0:16 * nl, :], [], ["ti"], "lt")
        dma("s", T.ti[16 * h + 8 + r0:16 * h + 16, :], T.rho[16 * r0:128, :], [], ["ti"], "lt")
    dma("y", T.ti[8:64:16, :], T.idt[0:64, :], ["idt"], ["ti"], "lt")
    dma("s", T.ti[71:128:16, :], T.idt[64:128, :], ["idt"], ["ti"], "lt")
    dma("y", u8(T.wq[:, :]), T.wc[:], [], ["wq"], "lw")
    dma("y", T.wp[:], T.ws[:], [], ["wq"], "lw")
    dma("y", T.vv[:], T.v[:], [], ["vv"], "lv")

    W_ = {"odd": (0, 6, [[16, 6]]), "even": (6, 6, [[32, 3], [96, 2]]), "t": (12, 16, [[1, 8], [0, 2]]), "e": (28, 2, [[8, 2]])}

    def W(n):
        return T.fw[:, W_[n][0]:W_[n][0] + W_[n][1]]
    for n in ("odd", "even"):
        iota(W(n), W_[n][2], 0, 0, ["w" + n])
    iota(T.c3[:, :], [[3, 96]], 1, 0, ["c30"])
    for n in ("t", "e"):
        iota(W(n), W_[n][2], 0, 0, ["w" + n])
    iota(T.tw[:, 0:1056:3], [[0, C]], 0, 0, ["twz"])
    op("v", V.memset, (T.one[:], 1.0), [], ["one"])
    col = {}

    def F(n):
        return T.cf[:, col[n]:col[n] + 1]

    def const(n, a, s1, s2=None, o0=A.add, o1=None):
        col[n] = len(col)
        ts(F(n), F(a), F(s1) if s1 in col else s1, F(s2) if s2 in col else s2, o0, o1, [k for k in (a, s1, s2) if k in col], [n])
    SR, AND = A.logical_shift_right, A.bitwise_and
    ts(T.ci[:, 16:24], T.ci[:, 0:8], 7, None, AND, None, ["cu"], ["cu7"])
    parts = (("q", 0, 15), ("R", 6, 1), ("h", 4, 7), ("h3", 4, 3), ("a1", 5, 1), ("p32", 0, 31), ("q2", 1, 7), ("G", 4, 1), ("odd", 0, 1))
    for k, (n, sh, m) in enumerate(parts):
        col[n] = k
        ts(T.ci[:, 32 + k:33 + k], T.ci[:, 8:9], sh, m, SR, AND, ["p"], ["ci"])
        if k == 3:
            ts(T.ul[:, 0:8], T.ci[:, 16:24], 16.0, None, A.mult, None, ["cu7"], ["ul0"])
    tc(T.cf[:, 0:9], T.ci[:, 32:41], ["ci"], [n for n, sh, m in parts])
    quant(T.uq[:], T.us[:], T.ut[:], ["ut"], ["uq"])
    const("y", "q", "R", 8.0, A.add, A.is_equal)
    const("po", "h3", 96.0, "q", A.mult, A.add)
    const("pe", "a1", 192.0, "p32", A.mult, A.add)
    const("p3", "h3", 288.0, None, A.mult)

    def order_u(k):
        op("v", V.tensor_copy, (T.pq[:, 128 * k:128 * k + 128].bitcast(dt.uint32), T.uq[:, 0:128].bitcast(dt.uint32).indirect(T.ul[:, 8 * k:8 * k + 8])), ["uq", "ul%d" % k], ["pq%d" % k])
        act(T.ps[:, 128 * k:128 * k + 128], T.us[:, 0:128].indirect(T.ul[:, 8 * k:8 * k + 8]), ["uq", "ul%d" % k], ["pq%d" % k])
    order_u(0)
    for b in range(2):
        act(T.et[:, 512 * b:512 * b + 512], T.one[:], ["one"], ["etz"], scale=0.0)

    def pack_x(c):
        c0, c1 = XC[c]
        quant(T.xq[:, c0:c1], T.xs[:, c0:c1], T.xt[:, 4 * c0:4 * c1], ["xt%d" % c], ["xq%d" % c])

    def scores(c, kinds):
        c0, c1 = XC[c]
        for k in kinds:
            mm(2 * k + c, c1 - c0, T.pq[:, 128 * k:128 * k + 128], T.ps[:, 128 * k:128 * k + 128], T.xq[:, c0:c1], T.xs[:, c0:c1], ["pq%d" % k, "xq%d" % c])

    def bits(c):
        c0, c1 = XC[c]
        ts(T.sb[:, c0:c1], bank(c, c1 - c0), 0.0, None, A.is_le, None, ["b%d" % c], ["sb"])

    def first(c):
        c0, c1 = XC[c]
        ts(T.d0[:, 3 * c0 + 2:3 * c1:3], bank(4 + c, c1 - c0), F("thr"), F("half"), A.is_gt, A.subtract, ["b%d" % (4 + c), "thr", "half"], ["beta%d" % c])

    def colours(c):
        c0, c1 = XC[c]
        act(T.d0[:, 3 * c0 + 1:3 * c1:3], bank(2 + c, c1 - c0), ["b%d" % (2 + c), "sgn"], ["phi%d" % c], SIGN, bias=2.0 ** -94, scale=F("sgn"))

    def recolour(c):
        c0, c1 = XC[c]
        op("v", V.tensor_tensor_scan, (T.tw[:, 3 * c0:3 * c1], T.d0[:, 3 * c0:3 * c1], T.d1[:, 3 * c0:3 * c1], 0.0, A.mult, A.add),
           ["d0c", "phi%d" % c, "beta%d" % c, "d1b", "d1m", "d1n"], ["tw%d" % c])
    for c in range(2):
        pack_x(c)
        scores(c, [0])
    const("e", "y", -1.5, None, A.mult)
    const("q5", "q", 5.0, 16.0, A.min, A.mult)
    ts(T.mp[:, 0:6], W("odd"), F("po"), 351.0, A.add, A.min, ["wodd", "po"], ["mpo"])
    ts(T.gr[:, 0:6], W("even"), F("pe"), 351.0, A.add, A.min, ["weven", "pe"], ["me"])
    ts(T.c3[:], T.c3[:], F("p3"), 1054.0, A.add, A.min, ["c30", "p3"], ["c3"])
    const("sg", "R", -2.0, 1.0, A.mult, A.add)
    const("h24", "h", "e", 16.0, A.mult, A.mult)
    const("sb0", "R", 15.0, "q5", A.mult, A.add)
    const("scale", "e", 3.0, None, A.add)
    tc(T.mp[:, 6:12], T.gr[:, 0:6], ["me"], ["mpe"])
    for c in range(2):
        bits(c)
    const("even0", "h24", 1.0, None, A.add)
    const("odd0", "h24", "e", 1.0, A.add, A.add)
    ts(T.sel[:], W("t"), F("sg"), F("sb0"), A.mult, A.add, ["wt", "sg", "sb0"], ["sel"])
    const("q6", "q2", 5.0, 16.0, A.min, A.mult)

    def windows(rs):
        for r in rs:
            ts(T.tw[:, 3 * r + 2:1056:24], T.ti[:, 88 * r:88 * r + 44], F("scale"), F("even0"), A.mult, A.add, ["ti", "scale", "even0"], ["tw0", "tw1"])
            ts(T.tw[:, 3 * r + 1:1056:24], T.ti[:, 88 * r + 44:88 * r + 88], F("scale"), F("odd0"), A.mult, A.add, ["ti", "scale", "odd0"], ["tw0", "tw1"])

    def places(t, n=96):
        tc(T.off[:], T.zm[:, 0:n].indirect(T.sel[:, 2 * t:2 * t + 1]), ["zm", "sel"], ["off"])
    tt(T.gm[:, 0:96], T.sb[:].indirect(T.mp[:, 0:6]), T.c3[:], A.add, ["sb", "mpo", "c3"], ["gm"])
    windows((0, 1))
    turn(T.zm[:, 0:96], T.gm[:, 0:96], ["gm"], ["zm"])
    windows((2, 3))
    places(7)
    windows((4, 5, 6, 7))
    iota(T.lw[:, :], [[0, 768]], 1, 0, ["lwz"])
    iota(T.zb[:, 352:384], [[0, 32]], 0, 0, ["zbz"])
    op("g", g.affine_select, (T.eye[:], T.one[:, 0:128], [[-1, 128]], A.is_equal, 0.0, 0, 1), ["one"], ["eye"])
    iota(T.yw[:, :], [[1, 22], [22, 16]], 0, 0, ["yw0"])
    iota(T.lk[:, :], [[0, 704]], 0, 0, ["lkz"])
    iota(T.d0[:, 0:1056:3], [[0, C]], 0, 0, ["d0c"])

    def later(cost, fn, *a):
        spare.append((cost, lambda: fn(*a)))
    SMALL = 0.06
    later(SMALL, const, "s5", "R", 5.0, 5.0, A.mult, A.add)
    later(SMALL, lambda: op("v", V.memset, (T.ro[:], 0), [], ["roz"]))
    later(SMALL, const, "x", "R", -15.0, "q", A.mult, A.add)
    later(SMALL, lambda: ts(T.sel[:, 10:11], F("s5"), F("q6"), None, A.add, None, ["s5", "q6", "sel"], ["sel5"]))
    later(SMALL, lambda: ts(T.gr[:, 8:10], W("e"), F("q2"), 10.0, A.add, A.min, ["we", "q2"], ["fb"]))
    later(SMALL, const, "ne", "x", 0.0, None, A.not_equal)
    later(SMALL, const, "hm", "h", -3.5, None, A.add)
    later(SMALL, lambda: ts(T.gr[:, 10:12], T.gr[:, 8:10], 6.0, -6.0, A.is_ge, A.mult, ["fb"], ["f6"]))
    later(SMALL, const, "o16", "odd", 16.0, None, A.mult)
    later(SMALL, const, "hh", "hm", "hm", 12.0, A.mult, A.is_gt)
    later(SMALL, lambda: tt(T.gr[:, 12:14], T.gr[:, 8:10], T.gr[:, 10:12], A.add, ["fb", "f6"], ["f7"]))
    later(SMALL, const, "thr", "ne", 1e29, None, A.mult)
    later(SMALL, const, "half", "ne", 1.0, 0.5, A.add, A.mult)
    later(SMALL, lambda: ts(T.gr[:, 14:16], T.gr[:, 12:14], 3.0, -5.0, A.is_ge, A.mult, ["f7"], ["f8"]))
    later(SMALL, lambda: tt(T.gr[:, 16:18], T.gr[:, 12:14], T.gr[:, 8:10], A.add, ["f7", "fb"], ["f9"]))
    later(SMALL, const, "ff", "hh", -0.9375, 1.0, A.mult, A.add)
    later(SMALL, const, "fo", "hh", 352.0, None, A.mult)
    later(SMALL, lambda: tt(T.gr[:, 18:20], T.gr[:, 16:18], T.gr[:, 14:16], A.add, ["f9", "f8"], ["f10"]))
    later(SMALL, const, "hof", "G", 352.0, None, A.mult)
    later(SMALL, const, "msc", "ne", 0.5, None, A.mult)
    later(SMALL, lambda: ts(T.gr[:, 20:22], T.gr[:, 18:20], 32.0, F("o16"), A.mult, A.add, ["f10", "o16"], ["f11"]))
    later(SMALL, const, "bsc", "half", -1.0, 1.5, A.mult, A.add)
    later(SMALL, const, "sgn", "q", 8.0, 0.5, A.is_lt, A.subtract)
    later(SMALL, lambda: ts(T.fin[:], T.gr[:, 20:22], F("ff"), F("fo"), A.mult, A.add, ["f11", "ff", "fo"], ["fin"]))
    later(SMALL, lambda: ts(T.ci[:, 24:32], T.ci[:, 8:16], 7, None, AND, None, ["p"], ["cc7"]))
    later(SMALL, lambda: op("v", V.memset, (T.ul[:, 16:20], 0), [], ["ul2"]))
    later(SMALL, lambda: op("v", V.memset, (T.ul[:, 20:24], 112), [], ["ul2"]))
    later(SMALL, lambda: ts(T.ul[:, 8:16], T.ci[:, 24:32], 16.0, 1.0, A.mult, A.add, ["cc7"], ["ul1"]))
    later(SMALL, lambda: ts(T.mp[:, 12:18], T.gr[:, 0:6], 3.0, 2.0, A.mult, A.add, ["me"], ["mp0"]))

    def plane(t, b, c0=0, c1=C):
        return t[:, C * b + c0:C * b + c1]

    def inter(t, b, c0=0, c1=C):
        return t[:, 4 * c0 + b:4 * c1:4]

    def halves(k, o):
        lo, hi = 264 * k, 264 * k + 264
        if o == "sum":
            tt(T.sm[:, 88 * k:88 * k + 88], T.tw[:, lo + 1:hi:3], T.tw[:, lo + 2:hi:3], A.add, ["tw0", "tw1"], ["sm"])
        elif o == "diff":
            tt(T.d1[:, lo:hi:3], T.tw[:, lo + 1:hi:3], T.tw[:, lo + 2:hi:3], A.subtract, ["tw0", "tw1"], ["d1d"])
        else:
            tt(T.d1[:, lo:hi:3], T.tw[:, lo + 1:hi:3], T.d1[:, lo + 1:hi:3], A.subtract, ["tw0", "tw1", "d1m"], ["d1b"])

    for rnd in range(3):
        partner = T.cores[rank ^ STEP[rnd]]
        hop = "hop%d" % rnd
        act(T.bra[:], T.sb[:].indirect(T.mp[:, 6:12]), ["sb", "mpe"], ["bra"])
        act(T.brb[:], T.sb[:].indirect(T.mp[:, 0:6]), ["sb", "mpo"], ["brb"])
        for b in range(4):
            act(plane(T.xh, b), inter(T.xt, b), ["xt0", "xt1"], ["xh%d" % b], scale=0.5)
        act(T.xi[:], T.xt[:], ["xt0", "xt1"], ["xi"], scale=0.5)
        if rnd:
            for k in range(4):
                later(0.16, halves, k, "b")
        if rnd == 2:
            later(0.14, quant, T.zq[:], T.zs[:], T.vv[:], ["vv"], ["zq"])
        for t in range(6):
            name = "g%d" % t if t % 2 else "gm"
            gt, br = T[name][:, 0:96], "brb" if t % 2 else "bra"
            lst, key = (T.mp[:, 12:18], "mp0") if t == 0 and rnd else (T.off[:, 0:6], "off")
            tt(gt, T.tw[:].indirect(lst), T[br][:], A.add, ["tw0", "tw1", "twz", key, br], [name])
            if t % 2:
                for n, (q, to, d) in enumerate(((t, t + 1, 0), (t, t + 1, 16), (8, t, 0), (8, t, 16))):
                    p = 32 * (to // 2) + d
                    dma("ys"[n % 2] if t == 5 else "y", T.lw[p:p + 1, 384 * (to % 2):384 * (to % 2) + 384], T[name][q:64:16, :], [name, "lwz"], ["lw"], hop)
            gap()
            turn(T.zm[:, 0:96], gt, [name], ["zm"])
            gap()
            if t == 5:
                need("v", gens["sel5"][1])
            places(t)
            if t % 2:
                for j, to in ((15 - t, 6 - t), (7, 7 - t)):
                    p, s = 32 * (to // 2), to % 2
                    for a in range(2):
                        n = 6 - a
                        ts(T.ro[p:p + 32, 12 * a + s:12 * a + 2 * n:2], T.zm[64 + 32 * a:96 + 32 * a, j:16 * n:16], 1152.0 * s - 1.5, 1.0 / 3.0, A.add, A.mult, ["zm", "roz"], ["ro"])
            else:
                gap()
        act(T.gb[:], T.lw[:].indirect(T.ro[:]), ["lw", "lwz", "ro", "roz"], ["gb"], IDENT, scale=1.0 / 3.0, bias=-MID - 0.5)
        tc(T.gm[:], T.tw[:].indirect(T.off[:, 0:12]), ["tw0", "tw1", "twz", "off"], ["gm"])
        gap()
        turn(T.zm[:], T.gm[:], ["gm"], ["zm"])
        gap()
        for p, j, p0 in ((96, 6, 0), (0, 9, 64)):
            for a in range(2):
                ts(T.zb[p:p + 32, 352 + 12 * a:364 + 12 * a], T.zm[p0 + 32 * a:p0 + 32 * a + 32, j:192:16], -3.0 * MID - 1.0, 1.0 / 3.0, A.add, A.mult, ["zm", "zbz"], ["zbx"])
        turn(T.zb[:, 0:352], T.gb[:], ["gb"], ["zb"])
        gap()
        ki, kk = T["ki%d" % rnd], "ki%d" % rnd
        ts(T.ko[:], T.zb[:].indirect(T.fin[:]), float(MID), None, A.add, None, ["zb", "zbx", "zbz", "fin"], ["ko"])
        act(ki[:], T.zb[:].indirect(T.fin[:]), ["zb", "zbx", "zbz", "fin"], [kk])
        gap()
        rid, pid = topo.addr(partner)[0:2]
        mask = topo.mask(core, partner)
        ne = len(topo.engines(core, partner))
        hq, hs, aq, as_ = T["hq%d" % rnd], T["hs%d" % rnd], T["aq%d" % rnd], T["as%d" % rnd]

        def send(out, in_, sem, key):
            before("g", [key], [])
            g.remote_dma(out, in_, T.sem[sem], T.sem.snt, pid, rid, mask)
            total["snt"] = total.get("snt", 0) + ne
            total[sem] = total.get(sem, 0) + ne

        def send_h(c):
            c0, c1 = CH[c]
            quant(hq[:, c0:c1], hs[:, c0:c1], T.hl[:, 4 * c0:4 * c1], ["hl%d" % c], ["hq%d%d" % (rnd, c)])
            send(u8(aq[:, c0:c1]), u8(hq[:, c0:c1]), "arr%d%d" % (rnd, c), "hq%d%d" % (rnd, c))
            send(as_[:, c0:c1], hs[:, c0:c1], "arr%d%d" % (rnd, c), "hq%d%d" % (rnd, c))
        send(T["ka%d" % rnd][:], ki[:, 0:22], "ark%d" % rnd, kk)
        if rnd == 0:
            act(T.yw[:], T.yw[:], ["yw0", "hof"], ["yw"], IDENT, bias=F("hof"))
        act(T.gh[:], T.yw[:].indirect(T.ko[:, 0:22]), ["yw", "ko"], ["gh"])

        def make_v(c, b):
            c0, c1 = CH[c]
            tt(inter(T.vt, b, c0, c1), plane(T.xh, b).indirect(T.ko[:, c0 // 16:c1 // 16]), inter(T.xi, b, c0, c1), A.add, ["xh%d" % b, "xi", "ko"], ["vt%d" % c])

        def layer(c):
            c0, c1 = CH[c]
            quant(T.vq[:, c0:c1], T.vs[:, c0:c1], T.vt[:, 4 * c0:4 * c1], ["vt%d" % c], ["vq%d" % c])
            for b in range(4):
                mm(4 * c + b, c1 - c0, T.wq[:, 128 * b:128 * b + 128], T.wp[:, 128 * b:128 * b + 128], T.vq[:, c0:c1], T.vs[:, c0:c1], ["wq", "vq%d" % c])
                if c == 0 or b % 2:
                    act(inter(T.hl, b, c0, c1), bank(4 * c + b, c1 - c0), ["b%d" % (4 * c + b)], ["hl%d" % c], scale=0.03125)
        for b in range(4):
            make_v(0, b)
        make_v(1, 0)
        layer(0)
        for b in range(1, 4):
            make_v(1, b)
        turn(T.zh[:], T.gh[:], ["gh"], ["zh"])
        layer(1)
        tc(T.roe[:], T.zh[:, 0:352:16], ["zh"], ["roe"])
        send_h(0)
        for b in (0, 2):
            ts(inter(T.hl, b, CH[1][0], CH[1][1]), bank(4 + b, CH[1][1] - CH[1][0]), 0.03125, None, A.mult, None, ["b%d" % (4 + b)], ["hl1"])
        send_h(1)
        for d in (0, 16):
            need("y", [("ark%d" % rnd, None)])
            dma("y", T.lk[d:128:32, :], T["ka%d" % rnd][:], ["lkz"], ["lk"], "kop%d" % rnd)
        tc(T.ge[:], T.lk[:].indirect(T.roe[:]), ["lk", "lkz", "roe"], ["ge"])
        if rnd == 0:
            for b in (2, 3):
                act(T.et[:, 512 * b:512 * b + 512], T.one[:], ["one"], ["etz"], scale=0.0)
            for b in range(4):
                act(T.et[:, 512 * b + b:512 * b + 512:4], T.eye[:], ["eye", "etz"], ["et"])
            for o in ("sum", "diff"):
                for k in range(4):
                    later(0.16, halves, k, o)
            later(0.2, order_u, 1)
            later(0.2, order_u, 2)
        gap()
        turn(T.ze[:], T.ge[:], ["ge"], ["ze"])
        gap()
        ts(T.eo[:], T.ze[:, 0:352:16], float(MID), None, A.add, None, ["ze"], ["eo"])
        gap(9.0)
        if rnd == 0:
            quant(T.eq[:], T.es[:], T.et[:], ["et", "etz"], ["eq"])
            act(T.d1[:, 2:1056:3], T.sm[:], ["sm", "half"], ["d1n"], scale=F("half"))
            act(T.d1[:, 1:1056:3], T.sm[:], ["sm", "msc"], ["d1m"], scale=F("msc"))
            act(T.d1[:, 0:1056:3], T.d1[:, 0:1056:3], ["d1d", "bsc"], ["d1b"], scale=F("bsc"))
        for c, (c0, c1) in enumerate(CH):
            need("t", [("arr%d%d" % (rnd, c), None)])
            for b in range(4):
                mm(4 * c + b, c1 - c0, T.eq[:, 128 * b:128 * b + 128], T.es[:, 128 * b:128 * b + 128], aq[:, c0:c1], as_[:, c0:c1], ["eq"])
                if c == 0 or b % 2:
                    act(plane(T.dp, b, c0, c1), bank(4 * c + b, c1 - c0), ["b%d" % (4 * c + b)], ["dp%d" % b])
                else:
                    tc(plane(T.dp, b, c0, c1), bank(4 * c + b, c1 - c0), ["b%d" % (4 * c + b)], ["dp%d" % b])

        def make_x(c, b):
            c0, c1 = XC[c]
            tt(inter(T.xt, b, c0, c1), plane(T.dp, b).indirect(T.eo[:, c0 // 16:c1 // 16]), inter(T.vt, b, c0, c1), A.add, ["dp%d" % b, "eo", "vt0", "vt1"], ["xt%d" % c])
        more = rnd < 2
        for b in (0, 2, 1, 3):
            make_x(0, b)
        make_x(1, 0)
        pack_x(0)
        scores(0, [1, 2, 0] if more else [1])
        colours(0)
        for b in (2, 1, 3):
            make_x(1, b)
        if more:
            first(0)
        pack_x(1)
        scores(1, [1, 2, 0] if more else [1])
        colours(1)
        if more:
            bits(0)
        recolour(0)
        if more:
            first(1)
            bits(1)
            recolour(1)

    mm(4, C, T.zq[:], T.zs[:], T.xq[:], T.xs[:], ["zq", "xq0", "xq1"])
    dma("y", T.oc[:], u8(T.xq[:, :]), ["xq0", "xq1"], [], "outs")
    for k in range(4):
        dma("y", T.osc[4 * k:4 * k + 4, :], T.xs[32 * k:32 * k + 4, :], ["xq0", "xq1"], [], "outs")
    act(T.yt[:], bank(4, C), ["b4"], ["yt"])
    dma("s", T.y[:], T.yt[:], ["yt"], [], "outs")
    recolour(1)
    ts(T.lt[:, 0:704:2], T.tw[:, 2:1056:3], -1.0, 1.0 / 3.0, A.add, A.mult, ["tw0", "tw1"], ["lt"])
    ts(T.lt[:, 1:704:2], T.tw[:, 1:1056:3], -1.0, 1.0 / 3.0, A.add, A.mult, ["tw0", "tw1"], ["lt"])
    dma("y", T.lr[1:8, 0:704], T.lt[1:8, :], ["lt"], [], "outs")
    dma("s", T.lr[0:7, 704:1408], T.lt[72:79, :], ["lt"], [], "outs")
    dma("y", T.lr[0:1, 0:704], T.lt[64:65, :], ["lt"], [], "outs")
    dma("s", T.lr[7:8, 704:1408], T.lt[15:16, :], ["lt"], [], "outs")
    need("g", [(s, None) for s in total if not s.startswith("ar")])
